import numpy as np
import ml_dtypes


def mxq(x, axis, fmt="e4m3"):
    dtype, down = {"e4m3": (ml_dtypes.float8_e4m3fn, 7), "e5m2": (ml_dtypes.float8_e5m2, 14)}[fmt]
    v = np.moveaxis(np.asarray(x, np.float32).astype(ml_dtypes.bfloat16).astype(np.float64), axis, -1)
    blocks = v.reshape(v.shape[:-1] + (-1, 32))
    amax = np.abs(blocks).max(-1, keepdims=True)
    byte = np.maximum(np.where(amax > 0, np.frexp(amax)[1] - 1 + 127, 0) - down, 1)
    scale = np.exp2(byte - 127.0)
    codes = (blocks / scale).astype(np.float32).astype(dtype).astype(np.float64)
    return np.moveaxis((codes * scale).reshape(v.shape), -1, axis)


WIDE = False


def mx_kscale(k):
    if not WIDE:
        return np.ones(k)
    levels = np.array([10, -10, 5, -5, 0])
    if k % 512:
        return np.exp2(np.random.permutation(np.resize(levels, k // 32))).repeat(32)
    a = np.empty((k // 512, 16))
    for p in range(k // 512):
        a[p, :8] = np.random.permutation(np.resize(levels, 8))
        for g in range(8):
            far = levels[np.abs(levels - a[p, g]) >= 10]
            a[p, g + 8] = far[np.random.randint(len(far))]
    return np.exp2(a.ravel()).repeat(32)


def f64(x):
    return np.asarray(x).astype(np.float64)


def striped(idx):
    return np.tile(idx.reshape(-1, 16).T, (8, 1)).astype(np.uint16)


def unstriped(offs):
    return offs[:16].T.reshape(-1).astype(np.int64)


E2M1 = np.array([0.0, 0.5, 1.0, 1.5, 2.0, 3.0, 4.0, 6.0, -0.0, -0.5, -1.0, -1.5, -2.0, -3.0, -4.0, -6.0])


def pack_weight(w, fmt):
    k, n = w.shape
    w = f64(np.asarray(w, np.float32).astype(ml_dtypes.bfloat16)).reshape(k // 32, 32, n)
    amax = np.abs(w).max(1)
    if fmt == "e4m3":
        byte = np.frexp(amax)[1] - 1 + 127 - 7
    else:
        mant, ex = np.frexp(amax / 6.0)
        byte = np.where(mant > 0.5, ex, ex - 1) + 127
    byte = np.clip(np.where(amax > 0, byte, 1), 1, 254)
    scaled = (w * np.exp2(127.0 - byte)[:, None, :]).reshape(k, n).astype(np.float32)
    by_word = np.ascontiguousarray(scaled.reshape(k // 512, 128, 4, n).transpose(0, 1, 3, 2))
    if fmt == "e4m3":
        words = by_word.astype(ml_dtypes.float8_e4m3fn).view(np.uint8)
    else:
        c = by_word.astype(ml_dtypes.float4_e2m1fn).view(np.uint8) & 0xF
        words = (c[..., 0::2] | (c[..., 1::2] << 4)).reshape(k // 512, 128, 2 * n)
    return np.ascontiguousarray(words), np.ascontiguousarray(byte.astype(np.uint8).reshape(k // 512, 16, n))


def unpack_weight(words, scales, fmt):
    g, _, n = scales.shape
    words = np.ascontiguousarray(words).reshape(g, 128, n, -1)
    if fmt == "e4m3":
        vals = words.view(ml_dtypes.float8_e4m3fn).astype(np.float64)
    else:
        nib = np.empty((g, 128, n, 4), np.uint8)
        nib[..., 0::2] = words & 0xF
        nib[..., 1::2] = words >> 4
        vals = E2M1[nib]
    vals = vals * np.repeat(np.exp2(scales.astype(np.float64) - 127.0), 8, axis=1)[..., None]
    return vals.transpose(0, 1, 3, 2).reshape(g * 512, n)


def gelu(v):
    return 0.5 * v * (1.0 + np.tanh(np.sqrt(2.0 / np.pi) * (v + 0.044715 * v**3)))


K, H, N, T, S, P = 1536, 1024, 256, 4096, 1024, 512

def setup_inputs():
    n = np.random.standard_normal
    s = mx_kscale(K)[:, None]
    u = mx_kscale(H)[:, None]
    d = {}
    d["tab_words"], d["tab_scales"] = pack_weight(n((K, T)) * s, "e2m1")
    d["offs"] = striped(np.random.permutation(T)[:S])
    d["pos1"] = striped(np.random.permutation(S)[:P])
    d["pos2"] = striped(np.random.permutation(S)[:P])
    d["w1"] = (n((K, H)) / K ** 0.5 / s * u.T).astype(np.float32)
    d["b1"] = (0.5 * n(H) * u[:, 0]).astype(np.float32)
    d["slope"] = (np.random.uniform(0.6, 2.0, H) / u[:, 0]).astype(np.float32)
    d["gain"] = (np.exp(0.5 * n(H)) * u[:, 0]).astype(np.float32)
    d["w2_words"], d["w2_scales"] = pack_weight(1.3 * n((H, H)) / H ** 0.5 / u * u.T, "e2m1")
    d["w3_words"], d["w3_scales"] = pack_weight(n((H, N)) / H ** 0.5 / u, "e4m3")
    d["b3"] = (0.5 * n(N)).astype(np.float32)
    return d

def reference(tab_words, tab_scales, offs, pos1, pos2, w1, b1, slope, gain,
              w2_words, w2_scales, w3_words, w3_scales, b3):
    v = unpack_weight(tab_words, tab_scales, "e2m1")[:, unstriped(offs)]
    h = (mxq(f64(w1), 0, "e4m3").T @ v) + f64(b1)[:, None]
    worst = np.maximum(h[:, unstriped(pos1)], h[:, unstriped(pos2)])
    bent = np.tanh(worst * f64(slope)[:, None]) * f64(gain)[:, None]
    w2 = unpack_weight(w2_words, w2_scales, "e2m1")
    full = worst + (w2.T @ mxq(bent, 0, "e4m3"))
    w3 = unpack_weight(w3_words, w3_scales, "e4m3")
    out = (w3.T @ mxq(full, 0, "e4m3")) + f64(b3)[:, None]
    return out

@@ -1,0 +1,361 @@
+from contextlib import ExitStack
+
+import concourse.mybir as mybir
+
+K, H, N, T, S, PAIRS = 1536, 1024, 256, 4096, 1024, 512
+FLOPS = 2 * (K * H * S + H * H * PAIRS + H * N * PAIRS)
+
+F32 = mybir.dt.float32
+BF16 = mybir.dt.bfloat16
+I32 = mybir.dt.int32
+U32 = mybir.dt.uint32
+U16 = mybir.dt.uint16
+U8 = mybir.dt.uint8
+FP8X4 = mybir.dt.float8_e4m3fn_x4
+FP4X4 = mybir.dt.float4_e2m1fn_x4
+ACT = mybir.ActivationFunctionType
+ALU = mybir.AluOpType
+
+P = 128
+PACK = 4
+PASS = P * PACK
+BANK = 512
+K_PASSES = K // PASS
+H_PASSES = H // PASS
+LIST_COL = 16
+SUB = 128
+PARKED = {1: 8, 2: 72}
+CHUNKS = ((0, 256), (256, 256))
+
+
+def tile_list_sewer_joint_grading_kernel(
+    tc, tab_words, tab_scales, offs, pos1, pos2, w1, b1, slope, gain,
+    w2_words, w2_scales, w3_words, w3_scales, b3, out,
+):
+    nc = tc.nc
+    with ExitStack() as ctx:
+        keep = ctx.enter_context(tc.tile_pool(name="keep", bufs=1))
+        psum = ctx.enter_context(tc.psum_pool(name="psum", bufs=8))
+
+        def held(shape, dtype, name):
+            return keep.tile(shape, dtype, name=name, align_bytes=64)
+
+        def in_slot(slot, shape, dtype, name):
+            return keep.tile(shape, dtype, name=name, tag="slot_" + slot, align_bytes=64)
+
+        scale_rows = in_slot("A", [P, T], U8, "scale_rows")
+        nc.vector.memset(scale_rows[:].bitcast(I32), 0)
+        warm_in = held([P, 1], F32, "warm_in")
+        nc.vector.memset(warm_in[:], 0.0)
+        picked_rows = held([P, S], U8, "picked_rows")
+        tab_planes = [picked_rows] + [held([P, S], U8, "tab_plane%d" % a) for a in range(1, K_PASSES)]
+        for plane in tab_planes[1:]:
+            nc.vector.memset(plane[:].bitcast(I32), 0)
+        w3_planes = held([P, H_PASSES * N], U8, "w3_planes")
+        nc.vector.memset(w3_planes[:].bitcast(I32), 0)
+
+        offs_t = keep.tile([P, S // LIST_COL], U16, name="offs_t")
+        nc.sync.dma_start(offs_t[:], offs)
+        tab_t = {}
+
+        def load_tab(a):
+            tab_t[a] = in_slot("BDB"[a], [P, T], U16, "tab%d" % a)
+            nc.sync.dma_start(out=tab_t[a][:].bitcast(I32), in_=tab_words[a].bitcast(I32))
+
+        for q in range(4):
+            nc.sync.dma_start(
+                out=scale_rows[32 * q : 32 * q + 4, :].bitcast(I32), in_=tab_scales[0, 4 * q : 4 * q + 4, :].bitcast(I32)
+            )
+        for a in range(1, K_PASSES):
+            nc.sync.dma_start(out=scale_rows[PARKED[a] : PARKED[a] + 16, :].bitcast(I32), in_=tab_scales[a].bitcast(I32))
+        warm_out = in_slot("D", [P, 1], F32, "warm_out")
+        nc.scalar.activation(warm_out[:], warm_in[:], ACT.Tanh)
+
+        w1_raw = {}
+
+        def load_w1(a, b, slot, pieces):
+            width = PASS // pieces
+            raw = in_slot(slot, [P, pieces, PACK, width], F32, "w1_raw%d_%d" % (a, b))
+            for i in range(pieces):
+                c0 = b * PASS + i * width
+                src = w1[a * PASS : (a + 1) * PASS, c0 : c0 + width]
+                nc.sync.dma_start(out=raw[:, i], in_=src.rearrange("(p j) c -> p j c", j=PACK))
+                w1_raw[a, b, i * width] = raw[:, i]
+
+        pos1_t = keep.tile([P, PAIRS // LIST_COL], U16, name="pos1_t")
+        nc.sync.dma_start(pos1_t[:], pos1)
+        pos2_t = keep.tile([P, PAIRS // LIST_COL], U16, name="pos2_t")
+        nc.sync.dma_start(pos2_t[:], pos2)
+        load_tab(0)
+        load_w1(0, 0, "C", 1)
+        load_tab(1)
+
+        chan = {}
+        vectors = held([P, 4, H_PASSES, PACK], F32, "vectors")
+        for i, (name, vec) in enumerate((("b1", b1), ("slope", slope), ("gain", gain))):
+            chan[name] = vectors[:, i]
+            nc.gpsimd.dma_start(out=chan[name], in_=vec.rearrange("(b p t) -> p b t", p=P, t=PACK))
+        for q in range(4):
+            nc.gpsimd.dma_start(
+                out=w3_planes[32 * q : 32 * q + 4, :].bitcast(I32).rearrange("r (a c) -> r a c", a=H_PASSES),
+                in_=w3_scales[:, 4 * q : 4 * q + 4, :].bitcast(I32).rearrange("a r c -> r a c"),
+            )
+        b3_t = vectors[:, 3, 0, 0 : N // P]
+        with nc.allow_non_contiguous_dma(reason="one bias value to a partition"):
+            nc.gpsimd.dma_start(out=b3_t, in_=b3.rearrange("(c p) -> p c", p=P))
+
+        nc.vector.tensor_copy(picked_rows[:], scale_rows[:].indirect(offs_t[:]))
+
+        def move_plane(a):
+            for q in range(4):
+                src = picked_rows[PARKED[a] + 4 * q : PARKED[a] + 4 * q + 4, :]
+                nc.sync.dma_start(out=tab_planes[a][32 * q : 32 * q + 4, :].bitcast(I32), in_=src.bitcast(I32))
+
+        move_plane(1)
+        load_w1(1, 0, "A", 1)
+        move_plane(2)
+
+        picked = [held([P, S], U16, "picked%d" % a) for a in range(K_PASSES)]
+
+        def gather_tab(a):
+            nc.vector.tensor_copy(picked[a][:], tab_t[a][:].indirect(offs_t[:]))
+
+        w1_grouped, w1_codes, w1_planes = {}, {}, {}
+
+        def cast_w1(a, b, piece, t0, t1, copy, slot):
+            if (a, b, t0) not in w1_grouped:
+                w1_grouped[a, b, t0] = in_slot(slot, [P, (t1 - t0) * PASS], BF16, "w1_grouped%d_%d_%d" % (a, b, t0))
+            raw = w1_raw[a, b, piece]
+            m0, m1 = piece // PACK, (piece + raw.shape[2]) // PACK
+            dst = w1_grouped[a, b, t0][:].rearrange("p (t m j) -> p m j t", t=t1 - t0, j=PACK)[:, m0:m1]
+            copy(dst, raw.rearrange("p j (m t) -> p m j t", t=PACK)[:, :, :, t0:t1])
+
+        def quantise_w1(a, b, g0, t0, t1, slot=None):
+            name = "w1_codes%d_%d_%d" % (a, b, t0)
+            codes = in_slot(slot or name, [P, (t1 - t0) * P], U32, name)
+            plane = held([P, (t1 - t0) * P], U8, "w1_plane%d_%d_%d" % (a, b, t0))
+            nc.vector.quantize_mx(
+                out=codes[:].bitcast(FP8X4), scales=plane[:],
+                in_=w1_grouped[a, b, g0][:, (t0 - g0) * PASS : (t1 - g0) * PASS],
+            )
+            for t in range(t0, t1):
+                cols = slice((t - t0) * P, (t - t0 + 1) * P)
+                w1_codes[a, b, t] = codes[:, cols]
+                w1_planes[a, b, t] = plane[:, cols]
+
+        banks = {}
+
+        def first_product(a, b, t):
+            for half in range(S // BANK):
+                if a == 0:
+                    banks[b, t, half] = psum.tile([P, BANK], F32, name="bank")
+                cols = slice(half * BANK, (half + 1) * BANK)
+                nc.tensor.matmul_mx(
+                    out=banks[b, t, half][:],
+                    lhsT=w1_codes[a, b, t].bitcast(FP8X4), lhsT_scale=w1_planes[a, b, t],
+                    rhs=picked[a][:, cols].bitcast(FP4X4), rhs_scale=tab_planes[a][:, cols],
+                    start=(a == 0), stop=(a == K_PASSES - 1),
+                )
+
+        h = {}
+
+        def empty_h(b, t):
+            h[b, t] = held([P, S], F32, "h%d_%d" % (b, t))
+            bias = chan["b1"][:, b, t : t + 1]
+            for half in range(S // BANK):
+                dst = h[b, t][:, half * BANK : (half + 1) * BANK]
+                if (b, t, half) == (0, 0, 1):
+                    nc.vector.tensor_scalar(dst, banks[b, t, half][:], bias, None, ALU.add)
+                else:
+                    nc.scalar.activation(dst, banks[b, t, half][:], ACT.Identity, bias=bias)
+
+        last = K_PASSES - 1
+        gather_tab(0)
+        load_tab(last)
+        cast_w1(0, 0, 0, 0, PACK, nc.scalar.copy, "E")
+        load_w1(last, 0, "C", 2)
+        quantise_w1(0, 0, 0, 0, PACK)
+        load_w1(0, 1, "E", 1)
+        for t in range(PACK):
+            first_product(0, 0, t)
+        gather_tab(1)
+        gather_tab(last)
+        cast_w1(1, 0, 0, 0, 2, nc.vector.tensor_copy, "F")
+        cast_w1(1, 0, 0, 2, 4, nc.scalar.copy, "F2")
+        for t0 in (0, 2):
+            quantise_w1(1, 0, t0, t0, t0 + 2)
+        load_w1(1, 1, "F", 1)
+        for t in range(PACK):
+            first_product(1, 0, t)
+        for piece in (0, PASS // 2):
+            cast_w1(last, 0, piece, 0, 2, nc.vector.tensor_copy, "G")
+            cast_w1(last, 0, piece, 2, 4, nc.scalar.copy, "G2")
+        quantise_w1(last, 0, 0, 0, 1, "L")
+        quantise_w1(last, 0, 0, 1, 2)
+        quantise_w1(last, 0, 2, 2, 4)
+        load_w1(last, 1, "G", 1)
+        for t in range(PACK):
+            first_product(last, 0, t)
+            empty_h(0, t)
+        w2_planes_raw = in_slot("C", [P, H_PASSES * H], U8, "w2_planes_raw")
+        nc.vector.memset(w2_planes_raw[:].bitcast(I32), 0)
+        for q in range(4):
+            nc.gpsimd.dma_start(
+                out=w2_planes_raw[32 * q : 32 * q + 4, :].bitcast(I32).rearrange("r (a c) -> r a c", a=H_PASSES),
+                in_=w2_scales[:, 4 * q : 4 * q + 4, :].bitcast(I32).rearrange("a r c -> r a c"),
+            )
+
+        worst_tiles, worst, bent_codes, bent_planes = {}, {}, {}, {}
+
+        def look_up(places, b, j0, width, t0, t1, slot):
+            found = in_slot(slot, [P, t1 - t0, width], F32, "found_" + slot)
+            cols = slice(j0 // LIST_COL, (j0 + width) // LIST_COL)
+            for t in range(t0, t1):
+                nc.vector.tensor_copy(found[:, t - t0, :], h[b, t][:].indirect(places[:, cols]))
+            return found
+
+        def meet(b, j0, width, t0, t1, up, down):
+            if (b, j0) not in worst_tiles:
+                worst_tiles[b, j0] = held([P, PACK, width], F32, "worst%d_%d" % (b, j0))
+                for s in range(0, width, SUB):
+                    worst[b, j0 + s] = worst_tiles[b, j0][:, :, s : s + SUB]
+            nc.vector.tensor_tensor(worst_tiles[b, j0][:, t0:t1, :], up[:], down[:], ALU.max)
+
+        flats = {}
+
+        def bend(b, j0, width, t0, t1):
+            curved = held([P, t1 - t0, width], F32, "curved%d_%d_%d" % (b, j0, t0))
+            if (b, j0) not in flats:
+                flats[b, j0] = held([P, PACK, width], BF16, "flat%d_%d" % (b, j0))
+            for t in range(t0, t1):
+                nc.scalar.activation(
+                    curved[:, t - t0, :], worst_tiles[b, j0][:, t, :], ACT.Tanh, scale=chan["slope"][:, b, t : t + 1]
+                )
+            for t in range(t0, t1):
+                nc.scalar.activation(
+                    flats[b, j0][:, t, :], curved[:, t - t0, :], ACT.Copy, scale=chan["gain"][:, b, t : t + 1]
+                )
+
+        def quantise_bent(b, j0, width, slot):
+            grouped = in_slot(slot, [P, width, PACK], BF16, "bent_grouped%d_%d" % (b, j0))
+            nc.vector.tensor_copy(
+                grouped[:].rearrange("p (c i) t -> p c t i", i=PACK),
+                flats[b, j0][:].rearrange("p t (c i) -> p c t i", i=PACK),
+            )
+            codes = held([P, width], U32, "bent_codes%d_%d" % (b, j0))
+            plane = held([P, width], U8, "bent_plane%d_%d" % (b, j0))
+            nc.vector.quantize_mx(out=codes[:].bitcast(FP8X4), scales=plane[:], in_=grouped[:].rearrange("p j t -> p (j t)"))
+            for s in range(0, width, SUB):
+                bent_codes[b, j0 + s] = codes[:, s : s + SUB]
+                bent_planes[b, j0 + s] = plane[:, s : s + SUB]
+
+        mix = {}
+
+        def second_product(a, b, j):
+            if a == 0:
+                mix[b, j] = psum.tile([P, PACK, SUB], F32, name="bank")
+            for t in range(PACK):
+                c0 = a * H + b * PASS + t * P
+                nc.tensor.matmul_mx(
+                    out=mix[b, j][:, t, :],
+                    lhsT=w2_codes[:, c0 : c0 + P].bitcast(FP4X4), lhsT_scale=w2_planes[:, c0 : c0 + P],
+                    rhs=bent_codes[a, j].bitcast(FP8X4), rhs_scale=bent_planes[a, j],
+                    start=(a == 0 and t == 0), stop=(a == H_PASSES - 1 and t == PACK - 1),
+                )
+
+        def finish(j0, width):
+            full_codes, full_planes = [], []
+            for b in range(H_PASSES):
+                grouped = held([P, width, PACK], BF16, "full_grouped%d_%d" % (b, j0))
+                for s in range(0, width, SUB):
+                    nc.vector.tensor_tensor(
+                        grouped[:, s : s + SUB, :].rearrange("p (c i) t -> p c t i", i=PACK),
+                        mix[b, j0 + s][:].rearrange("p t (c i) -> p c t i", i=PACK),
+                        worst[b, j0 + s].rearrange("p t (c i) -> p c t i", i=PACK),
+                        ALU.add,
+                    )
+                codes = held([P, width], U32, "full_codes%d_%d" % (b, j0))
+                plane = held([P, width], U8, "full_plane%d_%d" % (b, j0))
+                nc.vector.quantize_mx(out=codes[:].bitcast(FP8X4), scales=plane[:], in_=grouped[:].rearrange("p j t -> p (j t)"))
+                full_codes.append(codes)
+                full_planes.append(plane)
+            graded = psum.tile([P, N // P, width], F32, name="bank")
+            result = held([P, N // P, width], F32, "result%d" % j0)
+            for c in range(N // P):
+                for b in range(H_PASSES):
+                    c0 = b * N + c * P
+                    nc.tensor.matmul_mx(
+                        out=graded[:, c, :],
+                        lhsT=w3_codes[:, c0 : c0 + P].bitcast(FP8X4), lhsT_scale=w3_planes[:, c0 : c0 + P],
+                        rhs=full_codes[b][:].bitcast(FP8X4), rhs_scale=full_planes[b][:],
+                        start=(b == 0), stop=(b == H_PASSES - 1),
+                    )
+            for c in range(N // P):
+                nc.scalar.activation(result[:, c, :], graded[:, c, :], ACT.Identity, bias=b3_t[:, c : c + 1])
+            nc.sync.dma_start(out=out.rearrange("(c p) j -> p c j", p=P)[:, :, j0 : j0 + width], in_=result[:])
+
+        def first_half(t0, t1, up_slot, down_slot):
+            up = look_up(pos1_t, 0, 0, PAIRS, t0, t1, up_slot)
+            down = look_up(pos2_t, 0, 0, PAIRS, t0, t1, down_slot)
+            meet(0, 0, PAIRS, t0, t1, up, down)
+
+        first_half(0, PACK - 1, "up0", "down0")
+        for a in range(last):
+            cast_w1(a, 1, 0, 0, PACK, nc.scalar.copy, "LA"[a])
+            quantise_w1(a, 1, 0, 0, PACK)
+            for t in range(PACK):
+                first_product(a, 1, t)
+        first_half(PACK - 1, PACK, "L", "A")
+        for t0 in (0, 2):
+            cast_w1(last, 1, 0, t0, t0 + 2, nc.scalar.copy, ("D", "G2")[t0 // 2])
+            quantise_w1(last, 1, t0, t0, t0 + 2)
+        for t in range(PACK):
+            first_product(last, 1, t)
+            empty_h(1, t)
+
+        w2_raw = in_slot("E", [P, H_PASSES * H], U16, "w2_raw")
+        nc.sync.dma_start(
+            out=w2_raw[:].bitcast(I32).rearrange("p (a c) -> p a c", a=H_PASSES),
+            in_=w2_words.bitcast(I32).rearrange("a p c -> p a c"),
+        )
+        w3_codes = in_slot("F", [P, H_PASSES * N], I32, "w3_codes")
+        nc.sync.dma_start(
+            out=w3_codes[:].rearrange("p (a c) -> p a c", a=H_PASSES),
+            in_=w3_words.rearrange("a p c i -> p a (c i)").bitcast(I32),
+        )
+        w2_codes = in_slot("D", [P, H_PASSES * H], U16, "w2_codes")
+        nc.vector.tensor_copy(
+            w2_codes[:].rearrange("p (g t m) -> p g t m", t=PACK, m=P),
+            w2_raw[:].rearrange("p (g m t) -> p g t m", t=PACK, m=P),
+        )
+        w2_planes = in_slot("G2", [P, H_PASSES * H], U8, "w2_planes")
+        nc.vector.tensor_copy(
+            w2_planes[:].rearrange("p (g t m) -> p g t m", t=PACK, m=P),
+            w2_planes_raw[:].rearrange("p (g m t) -> p g t m", t=PACK, m=P),
+        )
+        for t0 in (0, 2):
+            bend(0, 0, PAIRS, t0, t0 + 2)
+
+        def second_half(j0, width, t0, t1, up_slot, down_slot):
+            up = look_up(pos1_t, 1, j0, width, t0, t1, up_slot)
+            down = look_up(pos2_t, 1, j0, width, t0, t1, down_slot)
+            meet(1, j0, width, t0, t1, up, down)
+            bend(1, j0, width, t0, t1)
+
+        def mix_chunk(a, j0, width):
+            for j in range(j0, j0 + width, SUB):
+                for b in range(H_PASSES):
+                    second_product(a, b, j)
+
+        (ja, wa), (jb, wb) = CHUNKS
+        second_half(ja, wa, 0, 4, "up0", "down0")
+        quantise_bent(0, 0, PAIRS, "up2")
+        mix_chunk(0, 0, PAIRS)
+        second_half(jb, wb, 0, 2, "up2", "down0")
+        quantise_bent(1, ja, wa, "down2")
+        mix_chunk(1, ja, wa)
+        second_half(jb, wb, 2, 4, "down2", "up0")
+        finish(ja, wa)
+        quantise_bent(1, jb, wb, "up1")
+        mix_chunk(1, jb, wb)
+        finish(jb, wb)

@@ -24,7 +24,6 @@ K_PASSES = K // PASS
 H_PASSES = H // PASS
 LIST_COL = 16
 SUB = 128
-PARKED = {1: 8, 2: 72}
 CHUNKS = ((0, 256), (256, 256))
 
 
@@ -45,14 +44,14 @@ def tile_list_sewer_joint_grading_kernel(
 
         scale_rows = in_slot("A", [P, T], U8, "scale_rows")
         nc.vector.memset(scale_rows[:].bitcast(I32), 0)
-        warm_in = held([P, 1], F32, "warm_in")
+        warm_in = in_slot("C", [P, 1], F32, "warm_in")
         nc.vector.memset(warm_in[:], 0.0)
         picked_rows = held([P, S], U8, "picked_rows")
         tab_planes = [picked_rows] + [held([P, S], U8, "tab_plane%d" % a) for a in range(1, K_PASSES)]
         for plane in tab_planes[1:]:
             nc.vector.memset(plane[:].bitcast(I32), 0)
-        w3_planes = held([P, H_PASSES * N], U8, "w3_planes")
-        nc.vector.memset(w3_planes[:].bitcast(I32), 0)
+        w2_plane1 = held([P, H], U8, "w2_plane1")
+        nc.vector.memset(w2_plane1[:].bitcast(I32), 0)
 
         offs_t = keep.tile([P, S // LIST_COL], U16, name="offs_t")
         nc.sync.dma_start(offs_t[:], offs)
@@ -62,12 +61,12 @@ def tile_list_sewer_joint_grading_kernel(
             tab_t[a] = in_slot("BDB"[a], [P, T], U16, "tab%d" % a)
             nc.sync.dma_start(out=tab_t[a][:].bitcast(I32), in_=tab_words[a].bitcast(I32))
 
-        for q in range(4):
+        for r in range(4):
             nc.sync.dma_start(
-                out=scale_rows[32 * q : 32 * q + 4, :].bitcast(I32), in_=tab_scales[0, 4 * q : 4 * q + 4, :].bitcast(I32)
+                out=scale_rows[r:P:16, :].bitcast(I32),
+                in_=tab_scales[0:2, r:16:4, :].bitcast(I32).rearrange("a q c -> q a c"),
             )
-        for a in range(1, K_PASSES):
-            nc.sync.dma_start(out=scale_rows[PARKED[a] : PARKED[a] + 16, :].bitcast(I32), in_=tab_scales[a].bitcast(I32))
+        nc.sync.dma_start(out=scale_rows[4:P:8, :].bitcast(I32), in_=tab_scales[2].bitcast(I32))
         warm_out = in_slot("D", [P, 1], F32, "warm_out")
         nc.scalar.activation(warm_out[:], warm_in[:], ACT.Tanh)
 
@@ -91,25 +90,16 @@ def tile_list_sewer_joint_grading_kernel(
         load_tab(1)
 
         chan = {}
-        vectors = held([P, 4, H_PASSES, PACK], F32, "vectors")
-        for i, (name, vec) in enumerate((("b1", b1), ("slope", slope), ("gain", gain))):
-            chan[name] = vectors[:, i]
-            nc.gpsimd.dma_start(out=chan[name], in_=vec.rearrange("(b p t) -> p b t", p=P, t=PACK))
-        for q in range(4):
-            nc.gpsimd.dma_start(
-                out=w3_planes[32 * q : 32 * q + 4, :].bitcast(I32).rearrange("r (a c) -> r a c", a=H_PASSES),
-                in_=w3_scales[:, 4 * q : 4 * q + 4, :].bitcast(I32).rearrange("a r c -> r a c"),
-            )
-        b3_t = vectors[:, 3, 0, 0 : N // P]
-        with nc.allow_non_contiguous_dma(reason="one bias value to a partition"):
-            nc.gpsimd.dma_start(out=b3_t, in_=b3.rearrange("(c p) -> p c", p=P))
+        b1_t = held([P, H_PASSES, PACK], F32, "b1_t")
+        chan["b1"] = b1_t[:]
+        nc.gpsimd.dma_start(out=b1_t[:], in_=b1.rearrange("(b p t) -> p b t", p=P, t=PACK))
 
         nc.vector.tensor_copy(picked_rows[:], scale_rows[:].indirect(offs_t[:]))
 
         def move_plane(a):
-            for q in range(4):
-                src = picked_rows[PARKED[a] + 4 * q : PARKED[a] + 4 * q + 4, :]
-                nc.sync.dma_start(out=tab_planes[a][32 * q : 32 * q + 4, :].bitcast(I32), in_=src.bitcast(I32))
+            for r in range(4):
+                src = picked_rows[(16 + r if a == 1 else 4 + 8 * r) : P : 32, :]
+                nc.sync.dma_start(out=tab_planes[a][r:P:32, :].bitcast(I32), in_=src.bitcast(I32))
 
         move_plane(1)
         load_w1(1, 0, "A", 1)
@@ -182,27 +172,50 @@ def tile_list_sewer_joint_grading_kernel(
         gather_tab(last)
         cast_w1(1, 0, 0, 0, 2, nc.vector.tensor_copy, "F")
         cast_w1(1, 0, 0, 2, 4, nc.scalar.copy, "F2")
-        for t0 in (0, 2):
-            quantise_w1(1, 0, t0, t0, t0 + 2)
+        quantise_w1(1, 0, 0, 0, 2)
         load_w1(1, 1, "F", 1)
-        for t in range(PACK):
+        for t in range(2):
             first_product(1, 0, t)
         for piece in (0, PASS // 2):
             cast_w1(last, 0, piece, 0, 2, nc.vector.tensor_copy, "G")
             cast_w1(last, 0, piece, 2, 4, nc.scalar.copy, "G2")
         quantise_w1(last, 0, 0, 0, 1, "L")
-        quantise_w1(last, 0, 0, 1, 2)
-        quantise_w1(last, 0, 2, 2, 4)
-        load_w1(last, 1, "G", 1)
-        for t in range(PACK):
+        quantise_w1(last, 0, 0, 1, 2, "M")
+        for t in range(2):
             first_product(last, 0, t)
             empty_h(0, t)
-        w2_planes_raw = in_slot("C", [P, H_PASSES * H], U8, "w2_planes_raw")
-        nc.vector.memset(w2_planes_raw[:].bitcast(I32), 0)
-        for q in range(4):
-            nc.gpsimd.dma_start(
-                out=w2_planes_raw[32 * q : 32 * q + 4, :].bitcast(I32).rearrange("r (a c) -> r a c", a=H_PASSES),
-                in_=w2_scales[:, 4 * q : 4 * q + 4, :].bitcast(I32).rearrange("a r c -> r a c"),
+        quantise_w1(1, 0, 2, 2, 4, "G")
+        quantise_w1(last, 0, 2, 2, 4)
+        for t in range(2, PACK):
+            first_product(1, 0, t)
+            first_product(last, 0, t)
+            empty_h(0, t)
+        w2_raw = in_slot("G", [P, H_PASSES * H], U16, "w2_raw")
+        nc.sync.dma_start(
+            out=w2_raw[:].bitcast(I32).rearrange("p (a c) -> p a c", a=H_PASSES),
+            in_=w2_words.bitcast(I32).rearrange("a p c -> p a c"),
+        )
+        load_w1(last, 1, "F2", 1)
+        vectors = in_slot("M", [P, 3, H_PASSES, PACK], F32, "vectors")
+        for i, (name, vec) in enumerate((("slope", slope), ("gain", gain))):
+            chan[name] = vectors[:, i]
+            nc.sync.dma_start(out=chan[name], in_=vec.rearrange("(b p t) -> p b t", p=P, t=PACK))
+        b3_t = vectors[:, 2, 0, 0 : N // P]
+        with nc.allow_non_contiguous_dma(reason="one bias value to a partition"):
+            nc.sync.dma_start(out=b3_t, in_=b3.rearrange("(c p) -> p c", p=P))
+        late_planes = in_slot("C", [P, H + H_PASSES * N], U8, "late_planes")
+        nc.vector.memset(late_planes[:].bitcast(I32), 0)
+        w2_rows = late_planes[:, 0:H]
+        w3_planes = late_planes[:, H:]
+        for r in range(4):
+            nc.sync.dma_start(
+                out=w2_rows[r:P:16, :].bitcast(I32),
+                in_=w2_scales[:, r:16:4, :].bitcast(I32).rearrange("a q c -> q a c"),
+            )
+        for r in range(4):
+            nc.sync.dma_start(
+                out=w3_planes[r:P:32, :].bitcast(I32).rearrange("q (a c) -> q a c", a=H_PASSES),
+                in_=w3_scales[:, r:16:4, :].bitcast(I32).rearrange("a q c -> q a c"),
             )
 
         worst_tiles, worst, bent_codes, bent_planes = {}, {}, {}, {}
@@ -216,15 +229,17 @@ def tile_list_sewer_joint_grading_kernel(
 
         def meet(b, j0, width, t0, t1, up, down):
             if (b, j0) not in worst_tiles:
-                worst_tiles[b, j0] = held([P, PACK, width], F32, "worst%d_%d" % (b, j0))
+                name = "worst%d_%d" % (b, j0)
+                worst_tiles[b, j0] = in_slot("F" if b == 0 else name, [P, PACK, width], F32, name)
                 for s in range(0, width, SUB):
                     worst[b, j0 + s] = worst_tiles[b, j0][:, :, s : s + SUB]
-            nc.vector.tensor_tensor(worst_tiles[b, j0][:, t0:t1, :], up[:], down[:], ALU.max)
+            nc.vector.tensor_tensor(worst_tiles[b, j0][:, t0:t1, :], up, down, ALU.max)
 
         flats = {}
 
         def bend(b, j0, width, t0, t1):
-            curved = held([P, t1 - t0, width], F32, "curved%d_%d_%d" % (b, j0, t0))
+            name = "curved%d_%d_%d" % (b, j0, t0)
+            curved = in_slot(name, [P, t1 - t0, width], F32, name)
             if (b, j0) not in flats:
                 flats[b, j0] = held([P, PACK, width], BF16, "flat%d_%d" % (b, j0))
             for t in range(t0, t1):
@@ -236,8 +251,8 @@ def tile_list_sewer_joint_grading_kernel(
                     flats[b, j0][:, t, :], curved[:, t - t0, :], ACT.Copy, scale=chan["gain"][:, b, t : t + 1]
                 )
 
-        def quantise_bent(b, j0, width, slot):
-            grouped = in_slot(slot, [P, width, PACK], BF16, "bent_grouped%d_%d" % (b, j0))
+        def quantise_bent(b, j0, width):
+            grouped = held([P, width, PACK], BF16, "bent_grouped%d_%d" % (b, j0))
             nc.vector.tensor_copy(
                 grouped[:].rearrange("p (c i) t -> p c t i", i=PACK),
                 flats[b, j0][:].rearrange("p t (c i) -> p c t i", i=PACK),
@@ -255,10 +270,10 @@ def tile_list_sewer_joint_grading_kernel(
             if a == 0:
                 mix[b, j] = psum.tile([P, PACK, SUB], F32, name="bank")
             for t in range(PACK):
-                c0 = a * H + b * PASS + t * P
+                c0 = b * PASS + t * P
                 nc.tensor.matmul_mx(
                     out=mix[b, j][:, t, :],
-                    lhsT=w2_codes[:, c0 : c0 + P].bitcast(FP4X4), lhsT_scale=w2_planes[:, c0 : c0 + P],
+                    lhsT=w2_codes[:, a * H + c0 : a * H + c0 + P].bitcast(FP4X4), lhsT_scale=w2_planes[a][:, c0 : c0 + P],
                     rhs=bent_codes[a, j].bitcast(FP8X4), rhs_scale=bent_planes[a, j],
                     start=(a == 0 and t == 0), stop=(a == H_PASSES - 1 and t == PACK - 1),
                 )
@@ -279,46 +294,46 @@ def tile_list_sewer_joint_grading_kernel(
                 nc.vector.quantize_mx(out=codes[:].bitcast(FP8X4), scales=plane[:], in_=grouped[:].rearrange("p j t -> p (j t)"))
                 full_codes.append(codes)
                 full_planes.append(plane)
-            graded = psum.tile([P, N // P, width], F32, name="bank")
-            result = held([P, N // P, width], F32, "result%d" % j0)
-            for c in range(N // P):
-                for b in range(H_PASSES):
+            graded = [psum.tile([P, width], F32, name="bank") for c in range(N // P)]
+            for b in range(H_PASSES):
+                for c in range(N // P):
                     c0 = b * N + c * P
                     nc.tensor.matmul_mx(
-                        out=graded[:, c, :],
+                        out=graded[c][:],
                         lhsT=w3_codes[:, c0 : c0 + P].bitcast(FP8X4), lhsT_scale=w3_planes[:, c0 : c0 + P],
                         rhs=full_codes[b][:].bitcast(FP8X4), rhs_scale=full_planes[b][:],
                         start=(b == 0), stop=(b == H_PASSES - 1),
                     )
+            result = held([P, N // P, width], F32, "result%d" % j0)
             for c in range(N // P):
-                nc.scalar.activation(result[:, c, :], graded[:, c, :], ACT.Identity, bias=b3_t[:, c : c + 1])
+                if c == 1 and j0 + width == PAIRS:
+                    nc.vector.tensor_scalar(result[:, c, :], graded[c][:], b3_t[:, c : c + 1], None, ALU.add)
+                else:
+                    nc.scalar.activation(result[:, c, :], graded[c][:], ACT.Identity, bias=b3_t[:, c : c + 1])
             nc.sync.dma_start(out=out.rearrange("(c p) j -> p c j", p=P)[:, :, j0 : j0 + width], in_=result[:])
 
-        def first_half(t0, t1, up_slot, down_slot):
-            up = look_up(pos1_t, 0, 0, PAIRS, t0, t1, up_slot)
-            down = look_up(pos2_t, 0, 0, PAIRS, t0, t1, down_slot)
-            meet(0, 0, PAIRS, t0, t1, up, down)
-
-        first_half(0, PACK - 1, "up0", "down0")
-        for a in range(last):
-            cast_w1(a, 1, 0, 0, PACK, nc.scalar.copy, "LA"[a])
-            quantise_w1(a, 1, 0, 0, PACK)
-            for t in range(PACK):
-                first_product(a, 1, t)
-        first_half(PACK - 1, PACK, "L", "A")
+        up0 = look_up(pos1_t, 0, 0, PAIRS, 0, PACK, "up0")
+        down0 = look_up(pos2_t, 0, 0, PAIRS, 0, PACK - 1, "down0")
+        cast_w1(0, 1, 0, 0, PACK, nc.scalar.copy, "L")
+        quantise_w1(0, 1, 0, 0, PACK)
+        for t in range(PACK):
+            first_product(0, 1, t)
+        down3 = look_up(pos2_t, 0, 0, PAIRS, PACK - 1, PACK, "E")
+        cast_w1(1, 1, 0, 0, PACK, nc.scalar.copy, "A")
+        quantise_w1(1, 1, 0, 0, PACK)
+        for t in range(PACK):
+            first_product(1, 1, t)
+        meet(0, 0, PAIRS, 0, PACK - 1, up0[:, 0 : PACK - 1, :], down0[:])
         for t0 in (0, 2):
             cast_w1(last, 1, 0, t0, t0 + 2, nc.scalar.copy, ("D", "G2")[t0 // 2])
-            quantise_w1(last, 1, t0, t0, t0 + 2)
+        quantise_w1(last, 1, 0, 0, 2)
+        meet(0, 0, PAIRS, PACK - 1, PACK, up0[:, PACK - 1 :, :], down3[:])
+        quantise_w1(last, 1, 2, 2, PACK)
         for t in range(PACK):
             first_product(last, 1, t)
             empty_h(1, t)
 
-        w2_raw = in_slot("E", [P, H_PASSES * H], U16, "w2_raw")
-        nc.sync.dma_start(
-            out=w2_raw[:].bitcast(I32).rearrange("p (a c) -> p a c", a=H_PASSES),
-            in_=w2_words.bitcast(I32).rearrange("a p c -> p a c"),
-        )
-        w3_codes = in_slot("F", [P, H_PASSES * N], I32, "w3_codes")
+        w3_codes = in_slot("F2", [P, H_PASSES * N], I32, "w3_codes")
         nc.sync.dma_start(
             out=w3_codes[:].rearrange("p (a c) -> p a c", a=H_PASSES),
             in_=w3_words.rearrange("a p c i -> p a (c i)").bitcast(I32),
@@ -328,19 +343,15 @@ def tile_list_sewer_joint_grading_kernel(
             w2_codes[:].rearrange("p (g t m) -> p g t m", t=PACK, m=P),
             w2_raw[:].rearrange("p (g m t) -> p g t m", t=PACK, m=P),
         )
-        w2_planes = in_slot("G2", [P, H_PASSES * H], U8, "w2_planes")
+        w2_planes = [in_slot("G2", [P, H], U8, "w2_plane0"), w2_plane1]
         nc.vector.tensor_copy(
-            w2_planes[:].rearrange("p (g t m) -> p g t m", t=PACK, m=P),
-            w2_planes_raw[:].rearrange("p (g m t) -> p g t m", t=PACK, m=P),
+            w2_planes[0][:].rearrange("p (g t m) -> p g t m", t=PACK, m=P),
+            w2_rows.rearrange("p (g m t) -> p g t m", t=PACK, m=P),
         )
+        for r in range(4):
+            nc.sync.dma_start(out=w2_plane1[r:P:32, :].bitcast(I32), in_=w2_planes[0][16 + r : P : 32, :].bitcast(I32))
         for t0 in (0, 2):
             bend(0, 0, PAIRS, t0, t0 + 2)
-
-        def second_half(j0, width, t0, t1, up_slot, down_slot):
-            up = look_up(pos1_t, 1, j0, width, t0, t1, up_slot)
-            down = look_up(pos2_t, 1, j0, width, t0, t1, down_slot)
-            meet(1, j0, width, t0, t1, up, down)
-            bend(1, j0, width, t0, t1)
 
         def mix_chunk(a, j0, width):
             for j in range(j0, j0 + width, SUB):
@@ -348,14 +359,24 @@ def tile_list_sewer_joint_grading_kernel(
                     second_product(a, b, j)
 
         (ja, wa), (jb, wb) = CHUNKS
-        second_half(ja, wa, 0, 4, "up0", "down0")
-        quantise_bent(0, 0, PAIRS, "up2")
-        mix_chunk(0, 0, PAIRS)
-        second_half(jb, wb, 0, 2, "up2", "down0")
-        quantise_bent(1, ja, wa, "down2")
+        up_a = look_up(pos1_t, 1, ja, wa, 0, PACK, "up0")
+        down_a = look_up(pos2_t, 1, ja, wa, 0, PACK, "down0")
+        meet(1, ja, wa, 0, PACK, up_a[:], down_a[:])
+        bend(1, ja, wa, 0, PACK)
+        down_b = look_up(pos2_t, 1, jb, wb, 0, PACK, "down0")
+        quantise_bent(0, 0, PAIRS)
+        up_b = look_up(pos1_t, 1, jb, wb, 0, 2, "curved0_0_2")
+        meet(1, jb, wb, 0, 2, up_b[:], down_b[:, 0:2, :])
+        bend(1, jb, wb, 0, 2)
+        mix_chunk(0, ja, wa)
+        quantise_bent(1, ja, wa)
         mix_chunk(1, ja, wa)
-        second_half(jb, wb, 2, 4, "down2", "up0")
-        finish(ja, wa)
-        quantise_bent(1, jb, wb, "up1")
+        mix_chunk(0, jb, wb)
+        up_b = look_up(pos1_t, 1, jb, wb, 2, PACK, "curved1_0_0")
+        meet(1, jb, wb, 2, PACK, up_b[:], down_b[:, 2:PACK, :])
+        bend(1, jb, wb, 2, PACK)
+        quantise_bent(1, jb, wb)
         mix_chunk(1, jb, wb)
-        finish(jb, wb)
+        finish(ja, wa)
+        for j in range(jb, jb + wb, SUB):
+            finish(j, SUB)

@@ -118,7 +118,9 @@ def tile_list_sewer_joint_grading_kernel(
             raw = w1_raw[a, b, piece]
             m0, m1 = piece // PACK, (piece + raw.shape[2]) // PACK
             dst = w1_grouped[a, b, t0][:].rearrange("p (t m j) -> p m j t", t=t1 - t0, j=PACK)[:, m0:m1]
-            copy(dst, raw.rearrange("p j (m t) -> p m j t", t=PACK)[:, :, :, t0:t1])
+            src = raw.rearrange("p j (m t) -> p m j t", t=PACK)[:, :, :, t0:t1]
+            for u in range(0, t1 - t0, 2):
+                copy(dst[:, :, :, u : u + 2], src[:, :, :, u : u + 2])
 
         def quantise_w1(a, b, g0, t0, t1, slot=None):
             name = "w1_codes%d_%d_%d" % (a, b, t0)
@@ -284,9 +286,9 @@ def tile_list_sewer_joint_grading_kernel(
                 grouped = held([P, width, PACK], BF16, "full_grouped%d_%d" % (b, j0))
                 for s in range(0, width, SUB):
                     nc.vector.tensor_tensor(
-                        grouped[:, s : s + SUB, :].rearrange("p (c i) t -> p c t i", i=PACK),
-                        mix[b, j0 + s][:].rearrange("p t (c i) -> p c t i", i=PACK),
-                        worst[b, j0 + s].rearrange("p t (c i) -> p c t i", i=PACK),
+                        grouped[:, s : s + SUB, :].rearrange("p (c i) t -> p c t i", i=2),
+                        mix[b, j0 + s][:].rearrange("p t (c i) -> p c t i", i=2),
+                        worst[b, j0 + s].rearrange("p t (c i) -> p c t i", i=2),
                         ALU.add,
                     )
                 codes = held([P, width], U32, "full_codes%d_%d" % (b, j0))

@@ -20,11 +20,35 @@ P = 128
 PACK = 4
 PASS = P * PACK
 BANK = 512
-K_PASSES = K // PASS
+BANKS = 8
+QUADRANT = 32
+LIVE = 4
+SCALE_ROWS = 16
+LIST_ROWS = 16
+LAST = K // PASS - 1
 H_PASSES = H // PASS
-LIST_COL = 16
-SUB = 128
-CHUNKS = ((0, 256), (256, 256))
+HALF = PACK // 2
+SUB = P
+EARLY, LATE = 0, PAIRS // 2
+RUN = PAIRS // 2
+
+SLOTS = (
+    ("scale_rows", "w1_raw 1 0", "w1_bf16 1 1 0"),
+    ("tab 0", "tab 2"),
+    ("zero_in", "w1_raw 0 0", "w1_raw 2 0", "late_planes"),
+    ("zero_bias", "tab 1", "w1_bf16 2 1 0", "w2_codes"),
+    ("w1_bf16 0 0 0", "w1_raw 0 1", "down 0 0 3"),
+    ("w1_bf16 1 0 0", "w1_raw 1 1", "worst 0 0"),
+    ("w1_bf16 1 0 2", "w1_raw 2 1", "w3_codes"),
+    ("w1_bf16 2 0 0", "w1_codes 1 0 2", "w2_raw"),
+    ("w1_bf16 2 0 2", "w1_bf16 2 1 2", "w2_plane 0"),
+    ("w1_codes 2 0 0", "w1_bf16 0 1 0"),
+    ("w1_codes 2 0 1", "vectors"),
+    ("up 0 0 0", "up 1 0 0"),
+    ("down 0 0 0", "down 1 0 0"),
+    ("curved 0 0 2", "up 1 %d 0" % LATE),
+    ("curved 1 0 0", "up 1 %d 2" % LATE),
+)
 
 
 def tile_list_sewer_joint_grading_kernel(
@@ -32,110 +56,107 @@ def tile_list_sewer_joint_grading_kernel(
     w2_words, w2_scales, w3_words, w3_scales, b3, out,
 ):
     nc = tc.nc
+    slot_of = {name: "slot%d" % number for number, tenants in enumerate(SLOTS) for name in tenants}
     with ExitStack() as ctx:
         keep = ctx.enter_context(tc.tile_pool(name="keep", bufs=1))
-        psum = ctx.enter_context(tc.psum_pool(name="psum", bufs=8))
+        psum = ctx.enter_context(tc.psum_pool(name="psum", bufs=BANKS))
 
-        def held(shape, dtype, name):
-            return keep.tile(shape, dtype, name=name, align_bytes=64)
+        def sbuf(shape, dtype, *key):
+            name = " ".join(str(part) for part in key)
+            label = name.replace(" ", "_")
+            return keep.tile(shape, dtype, name=label, tag=slot_of.get(name, label), align_bytes=64)
 
-        def in_slot(slot, shape, dtype, name):
-            return keep.tile(shape, dtype, name=name, tag="slot_" + slot, align_bytes=64)
+        def load_list(source, entries, name):
+            offsets = keep.tile([P, entries // LIST_ROWS], U16, name=name)
+            nc.sync.dma_start(offsets[:], source)
+            return offsets
 
-        scale_rows = in_slot("A", [P, T], U8, "scale_rows")
+        def load_two_passes(rows, scales):
+            for r in range(LIVE):
+                nc.sync.dma_start(
+                    out=rows[r : P : QUADRANT // 2, :].bitcast(I32),
+                    in_=scales[0:2, r:SCALE_ROWS:LIVE, :].bitcast(I32).rearrange("a q c -> q a c"),
+                )
+
+        def move_plane(plane, rows, first, step):
+            for r in range(LIVE):
+                source = rows[first + step * r : P : QUADRANT, :]
+                nc.sync.dma_start(out=plane[r:P:QUADRANT, :].bitcast(I32), in_=source.bitcast(I32))
+
+        scale_rows = sbuf([P, T], U8, "scale_rows")
         nc.vector.memset(scale_rows[:].bitcast(I32), 0)
-        warm_in = in_slot("C", [P, 1], F32, "warm_in")
-        nc.vector.memset(warm_in[:], 0.0)
-        picked_rows = held([P, S], U8, "picked_rows")
-        tab_planes = [picked_rows] + [held([P, S], U8, "tab_plane%d" % a) for a in range(1, K_PASSES)]
+        zero_in = sbuf([P, 1], F32, "zero_in")
+        nc.vector.memset(zero_in[:], 0.0)
+        zero_bias = sbuf([P, 1], F32, "zero_bias")
+        nc.vector.memset(zero_bias[:], 0.0)
+        picked_rows = sbuf([P, S], U8, "picked_rows")
+        tab_planes = [picked_rows] + [sbuf([P, S], U8, "tab_plane", a) for a in range(1, LAST + 1)]
         for plane in tab_planes[1:]:
             nc.vector.memset(plane[:].bitcast(I32), 0)
-        w2_plane1 = held([P, H], U8, "w2_plane1")
+        w2_plane1 = sbuf([P, H], U8, "w2_plane", 1)
         nc.vector.memset(w2_plane1[:].bitcast(I32), 0)
 
-        offs_t = keep.tile([P, S // LIST_COL], U16, name="offs_t")
-        nc.sync.dma_start(offs_t[:], offs)
-        tab_t = {}
+        offs_t = load_list(offs, S, "offs_t")
+        load_two_passes(scale_rows, tab_scales)
+        nc.sync.dma_start(out=scale_rows[LIVE : P : P // SCALE_ROWS, :].bitcast(I32), in_=tab_scales[LAST].bitcast(I32))
+
+        zero = sbuf([P, 1], F32, "zero")
+        nc.scalar.activation(zero[:], zero_in[:], ACT.Tanh, bias=zero_bias[:])
+
+        tab, w1_raw = {}, {}
 
         def load_tab(a):
-            tab_t[a] = in_slot("BDB"[a], [P, T], U16, "tab%d" % a)
-            nc.sync.dma_start(out=tab_t[a][:].bitcast(I32), in_=tab_words[a].bitcast(I32))
+            tab[a] = sbuf([P, T], U16, "tab", a)
+            nc.sync.dma_start(out=tab[a][:].bitcast(I32), in_=tab_words[a].bitcast(I32))
 
-        for r in range(4):
-            nc.sync.dma_start(
-                out=scale_rows[r:P:16, :].bitcast(I32),
-                in_=tab_scales[0:2, r:16:4, :].bitcast(I32).rearrange("a q c -> q a c"),
-            )
-        nc.sync.dma_start(out=scale_rows[4:P:8, :].bitcast(I32), in_=tab_scales[2].bitcast(I32))
-        warm_out = in_slot("D", [P, 1], F32, "warm_out")
-        nc.scalar.activation(warm_out[:], warm_in[:], ACT.Tanh)
+        def load_w1(a, b, parts=1):
+            width = PASS // parts
+            raw = sbuf([P, parts, PACK, width], F32, "w1_raw", a, b)
+            for part in range(parts):
+                c0 = part * width
+                source = w1[a * PASS : (a + 1) * PASS, b * PASS + c0 : b * PASS + c0 + width]
+                nc.sync.dma_start(out=raw[:, part], in_=source.rearrange("(p j) c -> p j c", j=PACK))
+                w1_raw[a, b, c0] = raw[:, part]
 
-        w1_raw = {}
-
-        def load_w1(a, b, slot, pieces):
-            width = PASS // pieces
-            raw = in_slot(slot, [P, pieces, PACK, width], F32, "w1_raw%d_%d" % (a, b))
-            for i in range(pieces):
-                c0 = b * PASS + i * width
-                src = w1[a * PASS : (a + 1) * PASS, c0 : c0 + width]
-                nc.sync.dma_start(out=raw[:, i], in_=src.rearrange("(p j) c -> p j c", j=PACK))
-                w1_raw[a, b, i * width] = raw[:, i]
-
-        pos1_t = keep.tile([P, PAIRS // LIST_COL], U16, name="pos1_t")
-        nc.sync.dma_start(pos1_t[:], pos1)
-        pos2_t = keep.tile([P, PAIRS // LIST_COL], U16, name="pos2_t")
-        nc.sync.dma_start(pos2_t[:], pos2)
+        pos1_t = load_list(pos1, PAIRS, "pos1_t")
+        pos2_t = load_list(pos2, PAIRS, "pos2_t")
         load_tab(0)
-        load_w1(0, 0, "C", 1)
+        load_w1(0, 0)
         load_tab(1)
-
-        chan = {}
-        b1_t = held([P, H_PASSES, PACK], F32, "b1_t")
-        chan["b1"] = b1_t[:]
+        b1_t = sbuf([P, H_PASSES, PACK], F32, "b1_t")
         nc.gpsimd.dma_start(out=b1_t[:], in_=b1.rearrange("(b p t) -> p b t", p=P, t=PACK))
 
         nc.vector.tensor_copy(picked_rows[:], scale_rows[:].indirect(offs_t[:]))
+        move_plane(tab_planes[1], picked_rows, QUADRANT // 2, 1)
+        load_w1(1, 0)
+        move_plane(tab_planes[LAST], picked_rows, LIVE, P // SCALE_ROWS)
 
-        def move_plane(a):
-            for r in range(4):
-                src = picked_rows[(16 + r if a == 1 else 4 + 8 * r) : P : 32, :]
-                nc.sync.dma_start(out=tab_planes[a][r:P:32, :].bitcast(I32), in_=src.bitcast(I32))
-
-        move_plane(1)
-        load_w1(1, 0, "A", 1)
-        move_plane(2)
-
-        picked = [held([P, S], U16, "picked%d" % a) for a in range(K_PASSES)]
+        picked = [sbuf([P, S], U16, "picked", a) for a in range(LAST + 1)]
 
         def gather_tab(a):
-            nc.vector.tensor_copy(picked[a][:], tab_t[a][:].indirect(offs_t[:]))
+            nc.vector.tensor_copy(picked[a][:], tab[a][:].indirect(offs_t[:]))
 
-        w1_grouped, w1_codes, w1_planes = {}, {}, {}
+        w1_bf16, w1_codes, w1_planes, banks, h = {}, {}, {}, {}, {}
 
-        def cast_w1(a, b, piece, t0, t1, copy, slot):
-            if (a, b, t0) not in w1_grouped:
-                w1_grouped[a, b, t0] = in_slot(slot, [P, (t1 - t0) * PASS], BF16, "w1_grouped%d_%d_%d" % (a, b, t0))
-            raw = w1_raw[a, b, piece]
-            m0, m1 = piece // PACK, (piece + raw.shape[2]) // PACK
-            dst = w1_grouped[a, b, t0][:].rearrange("p (t m j) -> p m j t", t=t1 - t0, j=PACK)[:, m0:m1]
-            src = raw.rearrange("p j (m t) -> p m j t", t=PACK)[:, :, :, t0:t1]
-            for u in range(0, t1 - t0, 2):
-                copy(dst[:, :, :, u : u + 2], src[:, :, :, u : u + 2])
+        def round_w1(a, b, c0, t0, t1, copy):
+            if (a, b, t0) not in w1_bf16:
+                w1_bf16[a, b, t0] = sbuf([P, (t1 - t0) * PASS], BF16, "w1_bf16", a, b, t0)
+            raw = w1_raw[a, b, c0]
+            m0, m1 = c0 // PACK, (c0 + raw.shape[2]) // PACK
+            rounded = w1_bf16[a, b, t0][:].rearrange("p (t m j) -> p m j t", t=t1 - t0, j=PACK)[:, m0:m1]
+            copy(rounded, raw.rearrange("p j (m t) -> p m j t", t=PACK)[:, :, :, t0:t1])
 
-        def quantise_w1(a, b, g0, t0, t1, slot=None):
-            name = "w1_codes%d_%d_%d" % (a, b, t0)
-            codes = in_slot(slot or name, [P, (t1 - t0) * P], U32, name)
-            plane = held([P, (t1 - t0) * P], U8, "w1_plane%d_%d_%d" % (a, b, t0))
+        def quantise_w1(a, b, tile_t0, t0, t1):
+            codes = sbuf([P, (t1 - t0) * P], U32, "w1_codes", a, b, t0)
+            plane = sbuf([P, (t1 - t0) * P], U8, "w1_plane", a, b, t0)
             nc.vector.quantize_mx(
                 out=codes[:].bitcast(FP8X4), scales=plane[:],
-                in_=w1_grouped[a, b, g0][:, (t0 - g0) * PASS : (t1 - g0) * PASS],
+                in_=w1_bf16[a, b, tile_t0][:, (t0 - tile_t0) * PASS : (t1 - tile_t0) * PASS],
             )
             for t in range(t0, t1):
                 cols = slice((t - t0) * P, (t - t0 + 1) * P)
                 w1_codes[a, b, t] = codes[:, cols]
                 w1_planes[a, b, t] = plane[:, cols]
-
-        banks = {}
 
         def first_product(a, b, t):
             for half in range(S // BANK):
@@ -146,144 +167,145 @@ def tile_list_sewer_joint_grading_kernel(
                     out=banks[b, t, half][:],
                     lhsT=w1_codes[a, b, t].bitcast(FP8X4), lhsT_scale=w1_planes[a, b, t],
                     rhs=picked[a][:, cols].bitcast(FP4X4), rhs_scale=tab_planes[a][:, cols],
-                    start=(a == 0), stop=(a == K_PASSES - 1),
+                    start=(a == 0), stop=(a == LAST),
                 )
 
-        h = {}
+        def add_bias(result, bank, bias, on_vector):
+            if on_vector:
+                nc.vector.tensor_scalar(result, bank, bias, None, ALU.add)
+            else:
+                nc.scalar.activation(result, bank, ACT.Identity, bias=bias)
 
         def empty_h(b, t):
-            h[b, t] = held([P, S], F32, "h%d_%d" % (b, t))
-            bias = chan["b1"][:, b, t : t + 1]
+            h[b, t] = sbuf([P, S], F32, "h", b, t)
             for half in range(S // BANK):
-                dst = h[b, t][:, half * BANK : (half + 1) * BANK]
-                if (b, t, half) == (0, 0, 1):
-                    nc.vector.tensor_scalar(dst, banks[b, t, half][:], bias, None, ALU.add)
-                else:
-                    nc.scalar.activation(dst, banks[b, t, half][:], ACT.Identity, bias=bias)
+                add_bias(
+                    h[b, t][:, half * BANK : (half + 1) * BANK], banks[b, t, half][:], b1_t[:, b, t : t + 1],
+                    on_vector=(b == 0 and t == 0 and half == 1),
+                )
 
-        last = K_PASSES - 1
         gather_tab(0)
-        load_tab(last)
-        cast_w1(0, 0, 0, 0, PACK, nc.scalar.copy, "E")
-        load_w1(last, 0, "C", 2)
+        load_tab(LAST)
+        round_w1(0, 0, 0, 0, PACK, nc.scalar.copy)
+        load_w1(LAST, 0, parts=2)
         quantise_w1(0, 0, 0, 0, PACK)
-        load_w1(0, 1, "E", 1)
+        load_w1(0, 1)
         for t in range(PACK):
             first_product(0, 0, t)
         gather_tab(1)
-        gather_tab(last)
-        cast_w1(1, 0, 0, 0, 2, nc.vector.tensor_copy, "F")
-        cast_w1(1, 0, 0, 2, 4, nc.scalar.copy, "F2")
-        quantise_w1(1, 0, 0, 0, 2)
-        load_w1(1, 1, "F", 1)
-        for t in range(2):
+        gather_tab(LAST)
+        round_w1(1, 0, 0, 0, HALF, nc.vector.tensor_copy)
+        round_w1(1, 0, 0, HALF, PACK, nc.scalar.copy)
+        quantise_w1(1, 0, 0, 0, HALF)
+        load_w1(1, 1)
+        for t in range(HALF):
             first_product(1, 0, t)
-        for piece in (0, PASS // 2):
-            cast_w1(last, 0, piece, 0, 2, nc.vector.tensor_copy, "G")
-            cast_w1(last, 0, piece, 2, 4, nc.scalar.copy, "G2")
-        quantise_w1(last, 0, 0, 0, 1, "L")
-        quantise_w1(last, 0, 0, 1, 2, "M")
-        for t in range(2):
-            first_product(last, 0, t)
+        for c0 in (0, PASS // 2):
+            round_w1(LAST, 0, c0, 0, HALF, nc.vector.tensor_copy)
+            round_w1(LAST, 0, c0, HALF, PACK, nc.scalar.copy)
+        for t in range(HALF):
+            quantise_w1(LAST, 0, 0, t, t + 1)
+        for t in range(HALF):
+            first_product(LAST, 0, t)
             empty_h(0, t)
-        quantise_w1(1, 0, 2, 2, 4, "G")
-        quantise_w1(last, 0, 2, 2, 4)
-        for t in range(2, PACK):
+        quantise_w1(1, 0, HALF, HALF, PACK)
+        quantise_w1(LAST, 0, HALF, HALF, PACK)
+        for t in range(HALF, PACK):
             first_product(1, 0, t)
-            first_product(last, 0, t)
+            first_product(LAST, 0, t)
             empty_h(0, t)
-        w2_raw = in_slot("G", [P, H_PASSES * H], U16, "w2_raw")
+
+        w2_raw = sbuf([P, H_PASSES * H], U16, "w2_raw")
         nc.sync.dma_start(
             out=w2_raw[:].bitcast(I32).rearrange("p (a c) -> p a c", a=H_PASSES),
             in_=w2_words.bitcast(I32).rearrange("a p c -> p a c"),
         )
-        load_w1(last, 1, "F2", 1)
-        vectors = in_slot("M", [P, 3, H_PASSES, PACK], F32, "vectors")
-        for i, (name, vec) in enumerate((("slope", slope), ("gain", gain))):
-            chan[name] = vectors[:, i]
-            nc.sync.dma_start(out=chan[name], in_=vec.rearrange("(b p t) -> p b t", p=P, t=PACK))
-        b3_t = vectors[:, 2, 0, 0 : N // P]
+        load_w1(LAST, 1)
+        vectors = sbuf([P, 3, H_PASSES, PACK], F32, "vectors")
+        slope_t, gain_t, b3_t = vectors[:, 0], vectors[:, 1], vectors[:, 2, 0, 0 : N // P]
+        for columns, values in ((slope_t, slope), (gain_t, gain)):
+            nc.sync.dma_start(out=columns, in_=values.rearrange("(b p t) -> p b t", p=P, t=PACK))
         with nc.allow_non_contiguous_dma(reason="one bias value to a partition"):
             nc.sync.dma_start(out=b3_t, in_=b3.rearrange("(c p) -> p c", p=P))
-        late_planes = in_slot("C", [P, H + H_PASSES * N], U8, "late_planes")
+        late_planes = sbuf([P, H + H_PASSES * N], U8, "late_planes")
         nc.vector.memset(late_planes[:].bitcast(I32), 0)
-        w2_rows = late_planes[:, 0:H]
-        w3_planes = late_planes[:, H:]
-        for r in range(4):
+        w2_rows, w3_planes = late_planes[:, 0:H], late_planes[:, H:]
+        load_two_passes(w2_rows, w2_scales)
+        for r in range(LIVE):
             nc.sync.dma_start(
-                out=w2_rows[r:P:16, :].bitcast(I32),
-                in_=w2_scales[:, r:16:4, :].bitcast(I32).rearrange("a q c -> q a c"),
-            )
-        for r in range(4):
-            nc.sync.dma_start(
-                out=w3_planes[r:P:32, :].bitcast(I32).rearrange("q (a c) -> q a c", a=H_PASSES),
-                in_=w3_scales[:, r:16:4, :].bitcast(I32).rearrange("a q c -> q a c"),
+                out=w3_planes[r:P:QUADRANT, :].bitcast(I32).rearrange("q (a c) -> q a c", a=H_PASSES),
+                in_=w3_scales[:, r:SCALE_ROWS:LIVE, :].bitcast(I32).rearrange("a q c -> q a c"),
             )
 
-        worst_tiles, worst, bent_codes, bent_planes = {}, {}, {}, {}
+        worst_tiles, worst, bent_bf16, bent_codes, bent_planes, mix = {}, {}, {}, {}, {}, {}
 
-        def look_up(places, b, j0, width, t0, t1, slot):
-            found = in_slot(slot, [P, t1 - t0, width], F32, "found_" + slot)
-            cols = slice(j0 // LIST_COL, (j0 + width) // LIST_COL)
+        def look_up(side, b, j0, width, t0, t1):
+            found = sbuf([P, t1 - t0, width], F32, side, b, j0, t0)
+            places = pos1_t if side == "up" else pos2_t
+            cols = slice(j0 // LIST_ROWS, (j0 + width) // LIST_ROWS)
             for t in range(t0, t1):
                 nc.vector.tensor_copy(found[:, t - t0, :], h[b, t][:].indirect(places[:, cols]))
             return found
 
         def meet(b, j0, width, t0, t1, up, down):
             if (b, j0) not in worst_tiles:
-                name = "worst%d_%d" % (b, j0)
-                worst_tiles[b, j0] = in_slot("F" if b == 0 else name, [P, PACK, width], F32, name)
+                worst_tiles[b, j0] = sbuf([P, PACK, width], F32, "worst", b, j0)
                 for s in range(0, width, SUB):
                     worst[b, j0 + s] = worst_tiles[b, j0][:, :, s : s + SUB]
             nc.vector.tensor_tensor(worst_tiles[b, j0][:, t0:t1, :], up, down, ALU.max)
 
-        flats = {}
-
         def bend(b, j0, width, t0, t1):
-            name = "curved%d_%d_%d" % (b, j0, t0)
-            curved = in_slot(name, [P, t1 - t0, width], F32, name)
-            if (b, j0) not in flats:
-                flats[b, j0] = held([P, PACK, width], BF16, "flat%d_%d" % (b, j0))
+            curved = sbuf([P, t1 - t0, width], F32, "curved", b, j0, t0)
+            if (b, j0) not in bent_bf16:
+                bent_bf16[b, j0] = sbuf([P, PACK, width], BF16, "bent_bf16", b, j0)
             for t in range(t0, t1):
                 nc.scalar.activation(
-                    curved[:, t - t0, :], worst_tiles[b, j0][:, t, :], ACT.Tanh, scale=chan["slope"][:, b, t : t + 1]
+                    curved[:, t - t0, :], worst_tiles[b, j0][:, t, :], ACT.Tanh,
+                    bias=zero[:], scale=slope_t[:, b, t : t + 1],
                 )
             for t in range(t0, t1):
                 nc.scalar.activation(
-                    flats[b, j0][:, t, :], curved[:, t - t0, :], ACT.Copy, scale=chan["gain"][:, b, t : t + 1]
+                    bent_bf16[b, j0][:, t, :], curved[:, t - t0, :], ACT.Copy, scale=gain_t[:, b, t : t + 1]
                 )
+
+        def quantise(grouped, width, *key):
+            codes = sbuf([P, width], U32, "codes", *key)
+            plane = sbuf([P, width], U8, "plane", *key)
+            nc.vector.quantize_mx(
+                out=codes[:].bitcast(FP8X4), scales=plane[:], in_=grouped[:].rearrange("p j t -> p (j t)")
+            )
+            return codes, plane
 
         def quantise_bent(b, j0, width):
-            grouped = held([P, width, PACK], BF16, "bent_grouped%d_%d" % (b, j0))
+            grouped = sbuf([P, width, PACK], BF16, "bent_grouped", b, j0)
             nc.vector.tensor_copy(
                 grouped[:].rearrange("p (c i) t -> p c t i", i=PACK),
-                flats[b, j0][:].rearrange("p t (c i) -> p c t i", i=PACK),
+                bent_bf16[b, j0][:].rearrange("p t (c i) -> p c t i", i=PACK),
             )
-            codes = held([P, width], U32, "bent_codes%d_%d" % (b, j0))
-            plane = held([P, width], U8, "bent_plane%d_%d" % (b, j0))
-            nc.vector.quantize_mx(out=codes[:].bitcast(FP8X4), scales=plane[:], in_=grouped[:].rearrange("p j t -> p (j t)"))
+            codes, plane = quantise(grouped, width, "bent", b, j0)
             for s in range(0, width, SUB):
                 bent_codes[b, j0 + s] = codes[:, s : s + SUB]
                 bent_planes[b, j0 + s] = plane[:, s : s + SUB]
 
-        mix = {}
-
-        def second_product(a, b, j):
-            if a == 0:
-                mix[b, j] = psum.tile([P, PACK, SUB], F32, name="bank")
-            for t in range(PACK):
-                c0 = b * PASS + t * P
-                nc.tensor.matmul_mx(
-                    out=mix[b, j][:, t, :],
-                    lhsT=w2_codes[:, a * H + c0 : a * H + c0 + P].bitcast(FP4X4), lhsT_scale=w2_planes[a][:, c0 : c0 + P],
-                    rhs=bent_codes[a, j].bitcast(FP8X4), rhs_scale=bent_planes[a, j],
-                    start=(a == 0 and t == 0), stop=(a == H_PASSES - 1 and t == PACK - 1),
-                )
+        def second_product(a, j0):
+            for j in range(j0, j0 + RUN, SUB):
+                for b in range(H_PASSES):
+                    if a == 0:
+                        mix[b, j] = psum.tile([P, PACK, SUB], F32, name="bank")
+                    for t in range(PACK):
+                        c0 = b * PASS + t * P
+                        nc.tensor.matmul_mx(
+                            out=mix[b, j][:, t, :],
+                            lhsT=w2_codes[:, a * H + c0 : a * H + c0 + P].bitcast(FP4X4),
+                            lhsT_scale=w2_planes[a][:, c0 : c0 + P],
+                            rhs=bent_codes[a, j].bitcast(FP8X4), rhs_scale=bent_planes[a, j],
+                            start=(a == 0 and t == 0), stop=(a == H_PASSES - 1 and t == PACK - 1),
+                        )
 
         def finish(j0, width):
-            full_codes, full_planes = [], []
+            full = []
             for b in range(H_PASSES):
-                grouped = held([P, width, PACK], BF16, "full_grouped%d_%d" % (b, j0))
+                grouped = sbuf([P, width, PACK], BF16, "full_grouped", b, j0)
                 for s in range(0, width, SUB):
                     nc.vector.tensor_tensor(
                         grouped[:, s : s + SUB, :].rearrange("p (c i) t -> p c t i", i=2),
@@ -291,94 +313,83 @@ def tile_list_sewer_joint_grading_kernel(
                         worst[b, j0 + s].rearrange("p t (c i) -> p c t i", i=2),
                         ALU.add,
                     )
-                codes = held([P, width], U32, "full_codes%d_%d" % (b, j0))
-                plane = held([P, width], U8, "full_plane%d_%d" % (b, j0))
-                nc.vector.quantize_mx(out=codes[:].bitcast(FP8X4), scales=plane[:], in_=grouped[:].rearrange("p j t -> p (j t)"))
-                full_codes.append(codes)
-                full_planes.append(plane)
+                full.append(quantise(grouped, width, "full", b, j0))
             graded = [psum.tile([P, width], F32, name="bank") for c in range(N // P)]
-            for b in range(H_PASSES):
+            for b, (codes, plane) in enumerate(full):
                 for c in range(N // P):
                     c0 = b * N + c * P
                     nc.tensor.matmul_mx(
                         out=graded[c][:],
                         lhsT=w3_codes[:, c0 : c0 + P].bitcast(FP8X4), lhsT_scale=w3_planes[:, c0 : c0 + P],
-                        rhs=full_codes[b][:].bitcast(FP8X4), rhs_scale=full_planes[b][:],
+                        rhs=codes[:].bitcast(FP8X4), rhs_scale=plane[:],
                         start=(b == 0), stop=(b == H_PASSES - 1),
                     )
-            result = held([P, N // P, width], F32, "result%d" % j0)
+            result = sbuf([P, N // P, width], F32, "result", j0)
             for c in range(N // P):
-                if c == 1 and j0 + width == PAIRS:
-                    nc.vector.tensor_scalar(result[:, c, :], graded[c][:], b3_t[:, c : c + 1], None, ALU.add)
-                else:
-                    nc.scalar.activation(result[:, c, :], graded[c][:], ACT.Identity, bias=b3_t[:, c : c + 1])
+                add_bias(result[:, c, :], graded[c][:], b3_t[:, c : c + 1], on_vector=(c == 1 and j0 + width == PAIRS))
             nc.sync.dma_start(out=out.rearrange("(c p) j -> p c j", p=P)[:, :, j0 : j0 + width], in_=result[:])
 
-        up0 = look_up(pos1_t, 0, 0, PAIRS, 0, PACK, "up0")
-        down0 = look_up(pos2_t, 0, 0, PAIRS, 0, PACK - 1, "down0")
-        cast_w1(0, 1, 0, 0, PACK, nc.scalar.copy, "L")
+        tail = PACK - 1
+        up0 = look_up("up", 0, 0, PAIRS, 0, PACK)
+        down0 = look_up("down", 0, 0, PAIRS, 0, tail)
+        round_w1(0, 1, 0, 0, PACK, nc.scalar.copy)
         quantise_w1(0, 1, 0, 0, PACK)
         for t in range(PACK):
             first_product(0, 1, t)
-        down3 = look_up(pos2_t, 0, 0, PAIRS, PACK - 1, PACK, "E")
-        cast_w1(1, 1, 0, 0, PACK, nc.scalar.copy, "A")
+        down0_tail = look_up("down", 0, 0, PAIRS, tail, PACK)
+        round_w1(1, 1, 0, 0, PACK, nc.scalar.copy)
         quantise_w1(1, 1, 0, 0, PACK)
         for t in range(PACK):
             first_product(1, 1, t)
-        meet(0, 0, PAIRS, 0, PACK - 1, up0[:, 0 : PACK - 1, :], down0[:])
-        for t0 in (0, 2):
-            cast_w1(last, 1, 0, t0, t0 + 2, nc.scalar.copy, ("D", "G2")[t0 // 2])
-        quantise_w1(last, 1, 0, 0, 2)
-        meet(0, 0, PAIRS, PACK - 1, PACK, up0[:, PACK - 1 :, :], down3[:])
-        quantise_w1(last, 1, 2, 2, PACK)
+        meet(0, 0, PAIRS, 0, tail, up0[:, 0:tail, :], down0[:])
+        for t0 in (0, HALF):
+            round_w1(LAST, 1, 0, t0, t0 + HALF, nc.scalar.copy)
+        quantise_w1(LAST, 1, 0, 0, HALF)
+        meet(0, 0, PAIRS, tail, PACK, up0[:, tail:, :], down0_tail[:])
+        quantise_w1(LAST, 1, HALF, HALF, PACK)
         for t in range(PACK):
-            first_product(last, 1, t)
+            first_product(LAST, 1, t)
             empty_h(1, t)
 
-        w3_codes = in_slot("F2", [P, H_PASSES * N], I32, "w3_codes")
+        w3_codes = sbuf([P, H_PASSES * N], I32, "w3_codes")
         nc.sync.dma_start(
             out=w3_codes[:].rearrange("p (a c) -> p a c", a=H_PASSES),
             in_=w3_words.rearrange("a p c i -> p a (c i)").bitcast(I32),
         )
-        w2_codes = in_slot("D", [P, H_PASSES * H], U16, "w2_codes")
+
+        w2_codes = sbuf([P, H_PASSES * H], U16, "w2_codes")
         nc.vector.tensor_copy(
             w2_codes[:].rearrange("p (g t m) -> p g t m", t=PACK, m=P),
             w2_raw[:].rearrange("p (g m t) -> p g t m", t=PACK, m=P),
         )
-        w2_planes = [in_slot("G2", [P, H], U8, "w2_plane0"), w2_plane1]
+        w2_planes = [sbuf([P, H], U8, "w2_plane", 0), w2_plane1]
         nc.vector.tensor_copy(
             w2_planes[0][:].rearrange("p (g t m) -> p g t m", t=PACK, m=P),
             w2_rows.rearrange("p (g m t) -> p g t m", t=PACK, m=P),
         )
-        for r in range(4):
-            nc.sync.dma_start(out=w2_plane1[r:P:32, :].bitcast(I32), in_=w2_planes[0][16 + r : P : 32, :].bitcast(I32))
-        for t0 in (0, 2):
-            bend(0, 0, PAIRS, t0, t0 + 2)
+        move_plane(w2_plane1, w2_planes[0], QUADRANT // 2, 1)
+        for t0 in (0, HALF):
+            bend(0, 0, PAIRS, t0, t0 + HALF)
 
-        def mix_chunk(a, j0, width):
-            for j in range(j0, j0 + width, SUB):
-                for b in range(H_PASSES):
-                    second_product(a, b, j)
-
-        (ja, wa), (jb, wb) = CHUNKS
-        up_a = look_up(pos1_t, 1, ja, wa, 0, PACK, "up0")
-        down_a = look_up(pos2_t, 1, ja, wa, 0, PACK, "down0")
-        meet(1, ja, wa, 0, PACK, up_a[:], down_a[:])
-        bend(1, ja, wa, 0, PACK)
-        down_b = look_up(pos2_t, 1, jb, wb, 0, PACK, "down0")
+        up_early = look_up("up", 1, EARLY, RUN, 0, PACK)
+        down1 = look_up("down", 1, 0, PAIRS, 0, PACK)
+        meet(1, EARLY, RUN, 0, PACK, up_early[:], down1[:, :, EARLY : EARLY + RUN])
+        bend(1, EARLY, RUN, 0, PACK)
+        down_late = down1[:, :, LATE : LATE + RUN]
         quantise_bent(0, 0, PAIRS)
-        up_b = look_up(pos1_t, 1, jb, wb, 0, 2, "curved0_0_2")
-        meet(1, jb, wb, 0, 2, up_b[:], down_b[:, 0:2, :])
-        bend(1, jb, wb, 0, 2)
-        mix_chunk(0, ja, wa)
-        quantise_bent(1, ja, wa)
-        mix_chunk(1, ja, wa)
-        mix_chunk(0, jb, wb)
-        up_b = look_up(pos1_t, 1, jb, wb, 2, PACK, "curved1_0_0")
-        meet(1, jb, wb, 2, PACK, up_b[:], down_b[:, 2:PACK, :])
-        bend(1, jb, wb, 2, PACK)
-        quantise_bent(1, jb, wb)
-        mix_chunk(1, jb, wb)
-        finish(ja, wa)
-        for j in range(jb, jb + wb, SUB):
+        up_late = look_up("up", 1, LATE, RUN, 0, HALF)
+        meet(1, LATE, RUN, 0, HALF, up_late[:], down_late[:, 0:HALF, :])
+        bend(1, LATE, RUN, 0, HALF)
+        second_product(0, EARLY)
+        quantise_bent(1, EARLY, RUN)
+        second_product(1, EARLY)
+        second_product(0, LATE)
+        up_last = look_up("up", 1, LATE, RUN, HALF, PACK)
+        for t in range(HALF, PACK):
+            meet(1, LATE, RUN, t, t + 1, up_last[:, t - HALF : t - HALF + 1, :], down_late[:, t : t + 1, :])
+            bend(1, LATE, RUN, t, t + 1)
+        quantise_bent(1, LATE, RUN)
+        second_product(1, LATE)
+        finish(EARLY, RUN)
+        for j in range(LATE, LATE + RUN, SUB):
             finish(j, SUB)

from contextlib import ExitStack

import concourse.mybir as mybir

K, H, N, T, S, PAIRS = 1536, 1024, 256, 4096, 1024, 512
FLOPS = 2 * (K * H * S + H * H * PAIRS + H * N * PAIRS)

F32 = mybir.dt.float32
BF16 = mybir.dt.bfloat16
I32 = mybir.dt.int32
U32 = mybir.dt.uint32
U16 = mybir.dt.uint16
U8 = mybir.dt.uint8
FP8X4 = mybir.dt.float8_e4m3fn_x4
FP4X4 = mybir.dt.float4_e2m1fn_x4
ACT = mybir.ActivationFunctionType
ALU = mybir.AluOpType

P = 128
PACK = 4
PASS = P * PACK
BANK = 512
BANKS = 8
QUADRANT = 32
LIVE = 4
SCALE_ROWS = 16
LIST_ROWS = 16
LAST = K // PASS - 1
H_PASSES = H // PASS
HALF = PACK // 2
SUB = P
EARLY, LATE = 0, PAIRS // 2
RUN = PAIRS // 2

SLOTS = (
    ("scale_rows", "w1_raw 1 0", "w1_bf16 1 1 0"),
    ("tab 0", "tab 2"),
    ("zero_in", "w1_raw 0 0", "w1_raw 2 0", "late_planes"),
    ("zero_bias", "tab 1", "w1_bf16 2 1 0", "w2_codes"),
    ("w1_bf16 0 0 0", "w1_raw 0 1", "down 0 0 3"),
    ("w1_bf16 1 0 0", "w1_raw 1 1", "worst 0 0"),
    ("w1_bf16 1 0 2", "w1_raw 2 1", "w3_codes"),
    ("w1_bf16 2 0 0", "w1_codes 1 0 2", "w2_raw"),
    ("w1_bf16 2 0 2", "w1_bf16 2 1 2", "w2_plane 0"),
    ("w1_codes 2 0 0", "w1_bf16 0 1 0"),
    ("w1_codes 2 0 1", "vectors"),
    ("up 0 0 0", "up 1 0 0"),
    ("down 0 0 0", "down 1 0 0"),
    ("curved 0 0 2", "up 1 %d 0" % LATE),
    ("curved 1 0 0", "up 1 %d 2" % LATE),
)


def tile_list_sewer_joint_grading_kernel(
    tc, tab_words, tab_scales, offs, pos1, pos2, w1, b1, slope, gain,
    w2_words, w2_scales, w3_words, w3_scales, b3, out,
):
    nc = tc.nc
    slot_of = {name: "slot%d" % number for number, tenants in enumerate(SLOTS) for name in tenants}
    with ExitStack() as ctx:
        keep = ctx.enter_context(tc.tile_pool(name="keep", bufs=1))
        psum = ctx.enter_context(tc.psum_pool(name="psum", bufs=BANKS))

        def sbuf(shape, dtype, *key):
            name = " ".join(str(part) for part in key)
            label = name.replace(" ", "_")
            return keep.tile(shape, dtype, name=label, tag=slot_of.get(name, label), align_bytes=64)

        def load_list(source, entries, name):
            offsets = keep.tile([P, entries // LIST_ROWS], U16, name=name)
            nc.sync.dma_start(offsets[:], source)
            return offsets

        def load_two_passes(rows, scales):
            for r in range(LIVE):
                nc.sync.dma_start(
                    out=rows[r : P : QUADRANT // 2, :].bitcast(I32),
                    in_=scales[0:2, r:SCALE_ROWS:LIVE, :].bitcast(I32).rearrange("a q c -> q a c"),
                )

        def move_plane(plane, rows, first, step):
            for r in range(LIVE):
                source = rows[first + step * r : P : QUADRANT, :]
                nc.sync.dma_start(out=plane[r:P:QUADRANT, :].bitcast(I32), in_=source.bitcast(I32))

        scale_rows = sbuf([P, T], U8, "scale_rows")
        nc.vector.memset(scale_rows[:].bitcast(I32), 0)
        zero_in = sbuf([P, 1], F32, "zero_in")
        nc.vector.memset(zero_in[:], 0.0)
        zero_bias = sbuf([P, 1], F32, "zero_bias")
        nc.vector.memset(zero_bias[:], 0.0)
        picked_rows = sbuf([P, S], U8, "picked_rows")
        tab_planes = [picked_rows] + [sbuf([P, S], U8, "tab_plane", a) for a in range(1, LAST + 1)]
        for plane in tab_planes[1:]:
            nc.vector.memset(plane[:].bitcast(I32), 0)
        w2_plane1 = sbuf([P, H], U8, "w2_plane", 1)
        nc.vector.memset(w2_plane1[:].bitcast(I32), 0)

        offs_t = load_list(offs, S, "offs_t")
        load_two_passes(scale_rows, tab_scales)
        nc.sync.dma_start(out=scale_rows[LIVE : P : P // SCALE_ROWS, :].bitcast(I32), in_=tab_scales[LAST].bitcast(I32))

        zero = sbuf([P, 1], F32, "zero")
        nc.scalar.activation(zero[:], zero_in[:], ACT.Tanh, bias=zero_bias[:])

        tab, w1_raw = {}, {}

        def load_tab(a):
            tab[a] = sbuf([P, T], U16, "tab", a)
            nc.sync.dma_start(out=tab[a][:].bitcast(I32), in_=tab_words[a].bitcast(I32))

        def load_w1(a, b, parts=1):
            width = PASS // parts
            raw = sbuf([P, parts, PACK, width], F32, "w1_raw", a, b)
            for part in range(parts):
                c0 = part * width
                source = w1[a * PASS : (a + 1) * PASS, b * PASS + c0 : b * PASS + c0 + width]
                nc.sync.dma_start(out=raw[:, part], in_=source.rearrange("(p j) c -> p j c", j=PACK))
                w1_raw[a, b, c0] = raw[:, part]

        pos1_t = load_list(pos1, PAIRS, "pos1_t")
        pos2_t = load_list(pos2, PAIRS, "pos2_t")
        load_tab(0)
        load_w1(0, 0)
        load_tab(1)
        b1_t = sbuf([P, H_PASSES, PACK], F32, "b1_t")
        nc.gpsimd.dma_start(out=b1_t[:], in_=b1.rearrange("(b p t) -> p b t", p=P, t=PACK))

        nc.vector.tensor_copy(picked_rows[:], scale_rows[:].indirect(offs_t[:]))
        move_plane(tab_planes[1], picked_rows, QUADRANT // 2, 1)
        load_w1(1, 0)
        move_plane(tab_planes[LAST], picked_rows, LIVE, P // SCALE_ROWS)

        picked = [sbuf([P, S], U16, "picked", a) for a in range(LAST + 1)]

        def gather_tab(a):
            nc.vector.tensor_copy(picked[a][:], tab[a][:].indirect(offs_t[:]))

        w1_bf16, w1_codes, w1_planes, banks, h = {}, {}, {}, {}, {}

        def round_w1(a, b, c0, t0, t1, copy):
            if (a, b, t0) not in w1_bf16:
                w1_bf16[a, b, t0] = sbuf([P, (t1 - t0) * PASS], BF16, "w1_bf16", a, b, t0)
            raw = w1_raw[a, b, c0]
            m0, m1 = c0 // PACK, (c0 + raw.shape[2]) // PACK
            rounded = w1_bf16[a, b, t0][:].rearrange("p (t m j) -> p m j t", t=t1 - t0, j=PACK)[:, m0:m1]
            copy(rounded, raw.rearrange("p j (m t) -> p m j t", t=PACK)[:, :, :, t0:t1])

        def quantise_w1(a, b, tile_t0, t0, t1):
            codes = sbuf([P, (t1 - t0) * P], U32, "w1_codes", a, b, t0)
            plane = sbuf([P, (t1 - t0) * P], U8, "w1_plane", a, b, t0)
            nc.vector.quantize_mx(
                out=codes[:].bitcast(FP8X4), scales=plane[:],
                in_=w1_bf16[a, b, tile_t0][:, (t0 - tile_t0) * PASS : (t1 - tile_t0) * PASS],
            )
            for t in range(t0, t1):
                cols = slice((t - t0) * P, (t - t0 + 1) * P)
                w1_codes[a, b, t] = codes[:, cols]
                w1_planes[a, b, t] = plane[:, cols]

        def first_product(a, b, t):
            for half in range(S // BANK):
                if a == 0:
                    banks[b, t, half] = psum.tile([P, BANK], F32, name="bank")
                cols = slice(half * BANK, (half + 1) * BANK)
                nc.tensor.matmul_mx(
                    out=banks[b, t, half][:],
                    lhsT=w1_codes[a, b, t].bitcast(FP8X4), lhsT_scale=w1_planes[a, b, t],
                    rhs=picked[a][:, cols].bitcast(FP4X4), rhs_scale=tab_planes[a][:, cols],
                    start=(a == 0), stop=(a == LAST),
                )

        def add_bias(result, bank, bias, on_vector):
            if on_vector:
                nc.vector.tensor_scalar(result, bank, bias, None, ALU.add)
            else:
                nc.scalar.activation(result, bank, ACT.Identity, bias=bias)

        def empty_h(b, t):
            h[b, t] = sbuf([P, S], F32, "h", b, t)
            for half in range(S // BANK):
                add_bias(
                    h[b, t][:, half * BANK : (half + 1) * BANK], banks[b, t, half][:], b1_t[:, b, t : t + 1],
                    on_vector=(b == 0 and t == 0 and half == 1),
                )

        gather_tab(0)
        load_tab(LAST)
        round_w1(0, 0, 0, 0, PACK, nc.scalar.copy)
        load_w1(LAST, 0, parts=2)
        quantise_w1(0, 0, 0, 0, PACK)
        load_w1(0, 1)
        for t in range(PACK):
            first_product(0, 0, t)
        gather_tab(1)
        gather_tab(LAST)
        round_w1(1, 0, 0, 0, HALF, nc.vector.tensor_copy)
        round_w1(1, 0, 0, HALF, PACK, nc.scalar.copy)
        quantise_w1(1, 0, 0, 0, HALF)
        load_w1(1, 1)
        for t in range(HALF):
            first_product(1, 0, t)
        for c0 in (0, PASS // 2):
            round_w1(LAST, 0, c0, 0, HALF, nc.vector.tensor_copy)
            round_w1(LAST, 0, c0, HALF, PACK, nc.scalar.copy)
        for t in range(HALF):
            quantise_w1(LAST, 0, 0, t, t + 1)
        for t in range(HALF):
            first_product(LAST, 0, t)
            empty_h(0, t)
        quantise_w1(1, 0, HALF, HALF, PACK)
        quantise_w1(LAST, 0, HALF, HALF, PACK)
        for t in range(HALF, PACK):
            first_product(1, 0, t)
            first_product(LAST, 0, t)
            empty_h(0, t)

        w2_raw = sbuf([P, H_PASSES * H], U16, "w2_raw")
        nc.sync.dma_start(
            out=w2_raw[:].bitcast(I32).rearrange("p (a c) -> p a c", a=H_PASSES),
            in_=w2_words.bitcast(I32).rearrange("a p c -> p a c"),
        )
        load_w1(LAST, 1)
        vectors = sbuf([P, 3, H_PASSES, PACK], F32, "vectors")
        slope_t, gain_t, b3_t = vectors[:, 0], vectors[:, 1], vectors[:, 2, 0, 0 : N // P]
        for columns, values in ((slope_t, slope), (gain_t, gain)):
            nc.sync.dma_start(out=columns, in_=values.rearrange("(b p t) -> p b t", p=P, t=PACK))
        with nc.allow_non_contiguous_dma(reason="one bias value to a partition"):
            nc.sync.dma_start(out=b3_t, in_=b3.rearrange("(c p) -> p c", p=P))
        late_planes = sbuf([P, H + H_PASSES * N], U8, "late_planes")
        nc.vector.memset(late_planes[:].bitcast(I32), 0)
        w2_rows, w3_planes = late_planes[:, 0:H], late_planes[:, H:]
        load_two_passes(w2_rows, w2_scales)
        for r in range(LIVE):
            nc.sync.dma_start(
                out=w3_planes[r:P:QUADRANT, :].bitcast(I32).rearrange("q (a c) -> q a c", a=H_PASSES),
                in_=w3_scales[:, r:SCALE_ROWS:LIVE, :].bitcast(I32).rearrange("a q c -> q a c"),
            )

        worst_tiles, worst, bent_bf16, bent_codes, bent_planes, mix = {}, {}, {}, {}, {}, {}

        def look_up(side, b, j0, width, t0, t1):
            found = sbuf([P, t1 - t0, width], F32, side, b, j0, t0)
            places = pos1_t if side == "up" else pos2_t
            cols = slice(j0 // LIST_ROWS, (j0 + width) // LIST_ROWS)
            for t in range(t0, t1):
                nc.vector.tensor_copy(found[:, t - t0, :], h[b, t][:].indirect(places[:, cols]))
            return found

        def meet(b, j0, width, t0, t1, up, down):
            if (b, j0) not in worst_tiles:
                worst_tiles[b, j0] = sbuf([P, PACK, width], F32, "worst", b, j0)
                for s in range(0, width, SUB):
                    worst[b, j0 + s] = worst_tiles[b, j0][:, :, s : s + SUB]
            nc.vector.tensor_tensor(worst_tiles[b, j0][:, t0:t1, :], up, down, ALU.max)

        def bend(b, j0, width, t0, t1):
            curved = sbuf([P, t1 - t0, width], F32, "curved", b, j0, t0)
            if (b, j0) not in bent_bf16:
                bent_bf16[b, j0] = sbuf([P, PACK, width], BF16, "bent_bf16", b, j0)
            for t in range(t0, t1):
                nc.scalar.activation(
                    curved[:, t - t0, :], worst_tiles[b, j0][:, t, :], ACT.Tanh,
                    bias=zero[:], scale=slope_t[:, b, t : t + 1],
                )
            for t in range(t0, t1):
                nc.scalar.activation(
                    bent_bf16[b, j0][:, t, :], curved[:, t - t0, :], ACT.Copy, scale=gain_t[:, b, t : t + 1]
                )

        def quantise(grouped, width, *key):
            codes = sbuf([P, width], U32, "codes", *key)
            plane = sbuf([P, width], U8, "plane", *key)
            nc.vector.quantize_mx(
                out=codes[:].bitcast(FP8X4), scales=plane[:], in_=grouped[:].rearrange("p j t -> p (j t)")
            )
            return codes, plane

        def quantise_bent(b, j0, width):
            grouped = sbuf([P, width, PACK], BF16, "bent_grouped", b, j0)
            nc.vector.tensor_copy(
                grouped[:].rearrange("p (c i) t -> p c t i", i=PACK),
                bent_bf16[b, j0][:].rearrange("p t (c i) -> p c t i", i=PACK),
            )
            codes, plane = quantise(grouped, width, "bent", b, j0)
            for s in range(0, width, SUB):
                bent_codes[b, j0 + s] = codes[:, s : s + SUB]
                bent_planes[b, j0 + s] = plane[:, s : s + SUB]

        def second_product(a, j0):
            for j in range(j0, j0 + RUN, SUB):
                for b in range(H_PASSES):
                    if a == 0:
                        mix[b, j] = psum.tile([P, PACK, SUB], F32, name="bank")
                    for t in range(PACK):
                        c0 = b * PASS + t * P
                        nc.tensor.matmul_mx(
                            out=mix[b, j][:, t, :],
                            lhsT=w2_codes[:, a * H + c0 : a * H + c0 + P].bitcast(FP4X4),
                            lhsT_scale=w2_planes[a][:, c0 : c0 + P],
                            rhs=bent_codes[a, j].bitcast(FP8X4), rhs_scale=bent_planes[a, j],
                            start=(a == 0 and t == 0), stop=(a == H_PASSES - 1 and t == PACK - 1),
                        )

        def finish(j0, width):
            full = []
            for b in range(H_PASSES):
                grouped = sbuf([P, width, PACK], BF16, "full_grouped", b, j0)
                for s in range(0, width, SUB):
                    nc.vector.tensor_tensor(
                        grouped[:, s : s + SUB, :].rearrange("p (c i) t -> p c t i", i=2),
                        mix[b, j0 + s][:].rearrange("p t (c i) -> p c t i", i=2),
                        worst[b, j0 + s].rearrange("p t (c i) -> p c t i", i=2),
                        ALU.add,
                    )
                full.append(quantise(grouped, width, "full", b, j0))
            graded = [psum.tile([P, width], F32, name="bank") for c in range(N // P)]
            for b, (codes, plane) in enumerate(full):
                for c in range(N // P):
                    c0 = b * N + c * P
                    nc.tensor.matmul_mx(
                        out=graded[c][:],
                        lhsT=w3_codes[:, c0 : c0 + P].bitcast(FP8X4), lhsT_scale=w3_planes[:, c0 : c0 + P],
                        rhs=codes[:].bitcast(FP8X4), rhs_scale=plane[:],
                        start=(b == 0), stop=(b == H_PASSES - 1),
                    )
            result = sbuf([P, N // P, width], F32, "result", j0)
            for c in range(N // P):
                add_bias(result[:, c, :], graded[c][:], b3_t[:, c : c + 1], on_vector=(c == 1 and j0 + width == PAIRS))
            nc.sync.dma_start(out=out.rearrange("(c p) j -> p c j", p=P)[:, :, j0 : j0 + width], in_=result[:])

        tail = PACK - 1
        up0 = look_up("up", 0, 0, PAIRS, 0, PACK)
        down0 = look_up("down", 0, 0, PAIRS, 0, tail)
        round_w1(0, 1, 0, 0, PACK, nc.scalar.copy)
        quantise_w1(0, 1, 0, 0, PACK)
        for t in range(PACK):
            first_product(0, 1, t)
        down0_tail = look_up("down", 0, 0, PAIRS, tail, PACK)
        round_w1(1, 1, 0, 0, PACK, nc.scalar.copy)
        quantise_w1(1, 1, 0, 0, PACK)
        for t in range(PACK):
            first_product(1, 1, t)
        meet(0, 0, PAIRS, 0, tail, up0[:, 0:tail, :], down0[:])
        for t0 in (0, HALF):
            round_w1(LAST, 1, 0, t0, t0 + HALF, nc.scalar.copy)
        quantise_w1(LAST, 1, 0, 0, HALF)
        meet(0, 0, PAIRS, tail, PACK, up0[:, tail:, :], down0_tail[:])
        quantise_w1(LAST, 1, HALF, HALF, PACK)
        for t in range(PACK):
            first_product(LAST, 1, t)
            empty_h(1, t)

        w3_codes = sbuf([P, H_PASSES * N], I32, "w3_codes")
        nc.sync.dma_start(
            out=w3_codes[:].rearrange("p (a c) -> p a c", a=H_PASSES),
            in_=w3_words.rearrange("a p c i -> p a (c i)").bitcast(I32),
        )

        w2_codes = sbuf([P, H_PASSES * H], U16, "w2_codes")
        nc.vector.tensor_copy(
            w2_codes[:].rearrange("p (g t m) -> p g t m", t=PACK, m=P),
            w2_raw[:].rearrange("p (g m t) -> p g t m", t=PACK, m=P),
        )
        w2_planes = [sbuf([P, H], U8, "w2_plane", 0), w2_plane1]
        nc.vector.tensor_copy(
            w2_planes[0][:].rearrange("p (g t m) -> p g t m", t=PACK, m=P),
            w2_rows.rearrange("p (g m t) -> p g t m", t=PACK, m=P),
        )
        move_plane(w2_plane1, w2_planes[0], QUADRANT // 2, 1)
        for t0 in (0, HALF):
            bend(0, 0, PAIRS, t0, t0 + HALF)

        up_early = look_up("up", 1, EARLY, RUN, 0, PACK)
        down1 = look_up("down", 1, 0, PAIRS, 0, PACK)
        meet(1, EARLY, RUN, 0, PACK, up_early[:], down1[:, :, EARLY : EARLY + RUN])
        bend(1, EARLY, RUN, 0, PACK)
        down_late = down1[:, :, LATE : LATE + RUN]
        quantise_bent(0, 0, PAIRS)
        up_late = look_up("up", 1, LATE, RUN, 0, HALF)
        meet(1, LATE, RUN, 0, HALF, up_late[:], down_late[:, 0:HALF, :])
        bend(1, LATE, RUN, 0, HALF)
        second_product(0, EARLY)
        quantise_bent(1, EARLY, RUN)
        second_product(1, EARLY)
        second_product(0, LATE)
        up_last = look_up("up", 1, LATE, RUN, HALF, PACK)
        for t in range(HALF, PACK):
            meet(1, LATE, RUN, t, t + 1, up_last[:, t - HALF : t - HALF + 1, :], down_late[:, t : t + 1, :])
            bend(1, LATE, RUN, t, t + 1)
        quantise_bent(1, LATE, RUN)
        second_product(1, LATE)
        finish(EARLY, RUN)
        for j in range(LATE, LATE + RUN, SUB):
            finish(j, SUB)
